import numpy as np
import ml_dtypes


def mxq(x, axis, fmt="e4m3"):
    dtype, down = {"e4m3": (ml_dtypes.float8_e4m3fn, 7), "e5m2": (ml_dtypes.float8_e5m2, 14)}[fmt]
    v = np.moveaxis(np.asarray(x, np.float32).astype(ml_dtypes.bfloat16).astype(np.float64), axis, -1)
    blocks = v.reshape(v.shape[:-1] + (-1, 32))
    amax = np.abs(blocks).max(-1, keepdims=True)
    byte = np.maximum(np.where(amax > 0, np.frexp(amax)[1] - 1 + 127, 0) - down, 1)
    scale = np.exp2(byte - 127.0)
    codes = (blocks / scale).astype(np.float32).astype(dtype).astype(np.float64)
    return np.moveaxis((codes * scale).reshape(v.shape), -1, axis)


WIDE = False


def mx_kscale(k):
    if not WIDE:
        return np.ones(k)
    levels = np.array([10, -10, 5, -5, 0])
    if k % 512:
        return np.exp2(np.random.permutation(np.resize(levels, k // 32))).repeat(32)
    a = np.empty((k // 512, 16))
    for p in range(k // 512):
        a[p, :8] = np.random.permutation(np.resize(levels, 8))
        for g in range(8):
            far = levels[np.abs(levels - a[p, g]) >= 10]
            a[p, g + 8] = far[np.random.randint(len(far))]
    return np.exp2(a.ravel()).repeat(32)


def f64(x):
    return np.asarray(x).astype(np.float64)


def striped(idx):
    return np.tile(idx.reshape(-1, 16).T, (8, 1)).astype(np.uint16)


def unstriped(offs):
    return offs[:16].T.reshape(-1).astype(np.int64)


E2M1 = np.array([0.0, 0.5, 1.0, 1.5, 2.0, 3.0, 4.0, 6.0, -0.0, -0.5, -1.0, -1.5, -2.0, -3.0, -4.0, -6.0])


def pack_weight(w, fmt):
    k, n = w.shape
    w = f64(np.asarray(w, np.float32).astype(ml_dtypes.bfloat16)).reshape(k // 32, 32, n)
    amax = np.abs(w).max(1)
    if fmt == "e4m3":
        byte = np.frexp(amax)[1] - 1 + 127 - 7
    else:
        mant, ex = np.frexp(amax / 6.0)
        byte = np.where(mant > 0.5, ex, ex - 1) + 127
    byte = np.clip(np.where(amax > 0, byte, 1), 1, 254)
    scaled = (w * np.exp2(127.0 - byte)[:, None, :]).reshape(k, n).astype(np.float32)
    by_word = np.ascontiguousarray(scaled.reshape(k // 512, 128, 4, n).transpose(0, 1, 3, 2))
    if fmt == "e4m3":
        words = by_word.astype(ml_dtypes.float8_e4m3fn).view(np.uint8)
    else:
        c = by_word.astype(ml_dtypes.float4_e2m1fn).view(np.uint8) & 0xF
        words = (c[..., 0::2] | (c[..., 1::2] << 4)).reshape(k // 512, 128, 2 * n)
    return np.ascontiguousarray(words), np.ascontiguousarray(byte.astype(np.uint8).reshape(k // 512, 16, n))


def unpack_weight(words, scales, fmt):
    g, _, n = scales.shape
    words = np.ascontiguousarray(words).reshape(g, 128, n, -1)
    if fmt == "e4m3":
        vals = words.view(ml_dtypes.float8_e4m3fn).astype(np.float64)
    else:
        nib = np.empty((g, 128, n, 4), np.uint8)
        nib[..., 0::2] = words & 0xF
        nib[..., 1::2] = words >> 4
        vals = E2M1[nib]
    vals = vals * np.repeat(np.exp2(scales.astype(np.float64) - 127.0), 8, axis=1)[..., None]
    return vals.transpose(0, 1, 3, 2).reshape(g * 512, n)


def gelu(v):
    return 0.5 * v * (1.0 + np.tanh(np.sqrt(2.0 / np.pi) * (v + 0.044715 * v**3)))


K, T, E, C, N = 1024, 1280, 8, 128, 128
K8 = 512


def by_expert(wq, xq):
    return np.concatenate([wq[e].T @ xq[:, e * C:(e + 1) * C] for e in range(E)], axis=1)


def setup_inputs():
    n = np.random.standard_normal
    s = mx_kscale(K)[:, None]
    w = n((E, K, N)) / np.sqrt(K) / s[None]
    w8 = [pack_weight(m[:K8], "e4m3") for m in w]
    w4 = [pack_weight(m[K8:], "e2m1") for m in w]
    return {
        "xT": (n((K, T)) * s).astype(np.float32),
        "xr": n((N, T)).astype(np.float32),
        "w8_words": np.stack([m[0] for m in w8]),
        "w8_scales": np.stack([m[1] for m in w8]),
        "w4_words": np.stack([m[0] for m in w4]),
        "w4_scales": np.stack([m[1] for m in w4]),
        "b": (0.3 * n((N, E))).astype(np.float32),
        "gate": np.tile(np.random.uniform(0.2, 1.0, E * C), (N, 1)).astype(np.float32),
        "offs": striped(np.random.permutation(T)[:E * C]),
    }


def reference(xT, xr, w8_words, w8_scales, w4_words, w4_scales, b, gate, offs):
    idx = unstriped(offs)
    w = np.stack([np.concatenate([unpack_weight(w8_words[e], w8_scales[e], "e4m3"), unpack_weight(w4_words[e], w4_scales[e], "e2m1")]) for e in range(E)])
    xq = mxq(f64(xT)[:, idx], 0, "e4m3")
    y = by_expert(w, xq)
    y = gelu(y + np.repeat(f64(b), C, axis=1))
    out = f64(xr).copy()
    out[:, idx] += f64(gate) * y
    return out

@@ -1,0 +1,181 @@
+from contextlib import ExitStack
+
+import concourse.mybir as mybir
+from concourse.masks import make_identity
+
+K, T, E, C, N = 1024, 1280, 8, 128, 128
+S = E * C
+FLOPS = 2 * S * K * N
+
+P = 128
+F32 = mybir.dt.float32
+BF16 = mybir.dt.bfloat16
+I32 = mybir.dt.int32
+U32 = mybir.dt.uint32
+U16 = mybir.dt.uint16
+U8 = mybir.dt.uint8
+FP8X4 = mybir.dt.float8_e4m3fn_x4
+FP4X4 = mybir.dt.float4_e2m1fn_x4
+COPY = mybir.ActivationFunctionType.Copy
+GELU = mybir.ActivationFunctionType.Gelu_apprx_tanh
+ADD = mybir.AluOpType.add
+MULT = mybir.AluOpType.mult
+
+
+def tile_moe_res_lin_gelu_kernel(
+    tc, xT, xr, w8_words, w8_scales, w4_words, w4_scales, b, gate, offs, out
+):
+    nc = tc.nc
+    with ExitStack() as ctx:
+        held = ctx.enter_context(tc.tile_pool(name="held", bufs=1))
+        psum = ctx.enter_context(tc.psum_pool(name="psum", bufs=1))
+
+        offsets = held.tile([P, S // 16], U16, name="offsets")
+        codes = [held.tile([P, T], U32, name=f"codes{a}", align_bytes=64) for a in range(2)]
+        planes = held.tile([P, T], U8, name="planes", align_bytes=64)
+        slot_codes = [held.tile([P, S], U32, name=f"slot_codes{a}", align_bytes=64) for a in range(2)]
+        slot_planes = held.tile([P, S], U8, name="slot_planes", align_bytes=64)
+        w8 = held.tile([P, E * 512], U8, name="w8", align_bytes=64)
+        w4 = held.tile([P, E * 256], U8, name="w4", align_bytes=64)
+        w8_plane = held.tile([P, E * N], U8, name="w8_plane", align_bytes=64)
+        w4_plane = held.tile([P, E * N], U8, name="w4_plane", align_bytes=64)
+        bias = held.tile([P, E], F32, name="bias")
+        gates = held.tile([P, S], F32, name="gates")
+        resid = held.tile([P, T], F32, name="resid")
+        y = held.tile([P, S], F32, name="y")
+        routed = held.tile([P, T], F32, name="routed")
+        total = held.tile([P, T], F32, name="total")
+        warm = held.tile([P, 8], F32, name="warm")
+        banks = [psum.tile([P, 512], F32, name=f"bank{e}") for e in range(4)]
+        NB = 4
+
+        nc.gpsimd.memset(warm[:], 0.0)
+        nc.gpsimd.memset(planes[:].bitcast(I32), 0)
+        nc.gpsimd.memset(w8_plane[:].bitcast(I32), 0)
+        nc.gpsimd.memset(w4_plane[:].bitcast(I32), 0)
+        nc.gpsimd.memset(routed[:], 0.0)
+        ident = held.tile([P, P], F32, name="ident")
+        make_identity(nc, ident[:])
+        nc.scalar.activation(warm[:], warm[:], GELU)
+
+        x_view = xT.rearrange("(a p j) w -> a p j w", a=2, p=P, j=4)
+        w8_view = w8_words.rearrange("e a p n r -> p (e a) (n r)").bitcast(I32)
+        w4_view = w4_words.rearrange("e a p n -> p (e a) n").bitcast(I32)
+        w8_i = w8[:].bitcast(I32).rearrange("p (e n) -> p e n", e=E)
+        w4_i = w4[:].bitcast(I32).rearrange("p (e n) -> p e n", e=E)
+
+        chunks = ((0, 0, 4, 0, 768), (0, 0, 4, 768, T), (1, 0, 4, 0, 512), (1, 0, 4, 512, 1024), (1, 0, 4, 1024, T))
+        raw = []
+        for i, (a, j, k, lo, hi) in enumerate(chunks):
+            tile = held.tile([P, k - j, hi - lo], F32, name=f"raw{i}")
+            nc.sync.dma_start(tile[:], x_view[a][:, j:k, lo:hi])
+            raw.append(tile)
+            if i == 0:
+                nc.sync.dma_start(offsets[:], offs)
+
+        def load_scales(plane, scales):
+            src = scales.rearrange("e a q n -> q (e a) n").bitcast(I32)
+            dst = plane[:].bitcast(I32).rearrange("p (e n) -> p e n", e=E)
+            for quad in range(4):
+                nc.sync.dma_start(dst[32 * quad : 32 * quad + 4], src[4 * quad : 4 * quad + 4])
+
+        def load_words(lo, hi):
+            nc.sync.dma_start(w8_i[:, lo:hi, :], w8_view[:, lo:hi, :])
+            nc.sync.dma_start(w4_i[:, lo:hi, :], w4_view[:, lo:hi, :])
+
+        load_scales(w8_plane, w8_scales)
+        load_scales(w4_plane, w4_scales)
+        nc.sync.dma_start(bias[:], b)
+        load_words(0, 4)
+        nc.sync.dma_start(gates[:], gate)
+        load_words(4, 8)
+        nc.sync.dma_start(resid[:], xr)
+
+        def copy(dst, src, vector):
+            if vector:
+                nc.vector.tensor_copy(dst, src)
+            else:
+                nc.scalar.activation(dst, src, COPY)
+
+        def cast_half(grouped, src, h, vector):
+            copy(grouped[:, :, 2 * h : 2 * h + 2], src.rearrange("p j w -> p w j"), vector)
+
+        def cast(grouped, src, vector):
+            copy(
+                grouped[:].rearrange("p (w i) j -> p w j i", i=4), src.rearrange("p j (w i) -> p w j i", i=4), vector
+            )
+
+        def quantise(grouped, a, lo, hi, base):
+            first = 4 * (1 - a)
+            nc.vector.quantize_mx(
+                codes[a][:, lo:hi].bitcast(FP8X4),
+                planes[first:P, lo:hi],
+                grouped[:, lo - base : hi - base, :].rearrange("p w j -> p (w j)"),
+            )
+
+        def gather(dst, src, lo, hi):
+            nc.vector.tensor_copy(dst[:, lo:hi], src[:].indirect(offsets[:, lo // 16 : hi // 16]))
+
+        def product(e, a):
+            slots = slice(e * C, (e + 1) * C)
+            if a == 0:
+                w = w8[:, 512 * e : 512 * (e + 1)].bitcast(FP8X4)
+                plane = w8_plane
+            else:
+                w = w4[:, 256 * e : 256 * (e + 1)].bitcast(FP4X4)
+                plane = w4_plane
+            nc.tensor.matmul_mx(
+                out=banks[e % NB][:, :C],
+                lhsT=w,
+                lhsT_scale=plane[:, e * N : (e + 1) * N],
+                rhs=slot_codes[a][:, slots].bitcast(FP8X4),
+                rhs_scale=slot_planes[4 * (1 - a) : P, slots],
+                start=(a == 0),
+                stop=(a == 1),
+            )
+
+        for i, (a, base, units) in enumerate((
+            (0, 0, ((512, 768, True), (0, 512, False))),
+            (0, 768, ((1024, 1280, True), (768, 1024, False))),
+            (1, 0, ((0, 512, False),)),
+            (1, 512, ((768, 1024, True), (512, 768, False))),
+            (1, 1024, ((1152, 1280, True), (1024, 1152, False))),
+        )):
+            for lo, hi, vector in units:
+                grouped = held.tile([P, hi - lo, 4], BF16, name=f"grouped{a}_{lo}", align_bytes=64)
+                cast(grouped, raw[i][:, :, lo - base : hi - base], vector)
+                quantise(grouped, a, lo, hi, lo)
+            if i == 1:
+                for lo in range(0, S, 512):
+                    gather(slot_codes[0], codes[0], lo, lo + 512)
+
+        for lo in range(0, S, 512):
+            gather(slot_planes, planes, lo, lo + 512)
+            gather(slot_codes[1], codes[1], lo, lo + 512)
+            for e in range(lo // C, (lo + 512) // C):
+                product(e, 0)
+            for e in range(lo // C, (lo + 512) // C):
+                product(e, 1)
+                nc.scalar.activation(y[:, e * C : (e + 1) * C], banks[e % NB][:, :C], GELU, bias=bias[:, e : e + 1])
+        V = 960
+        VT = 1024
+        flips = [psum.tile([P, 512], F32, name=f"flip{i}") for i in range(2)]
+        backs = [psum.tile([P, 512], F32, name=f"back{i}") for i in range(2)]
+        flipped = held.tile([P, VT], F32, name="flipped")
+        for i, lo in enumerate(range(0, VT, 512)):
+            hi = lo + 512
+            for c in range(lo, hi, P):
+                nc.tensor.transpose(flips[i][:, c - lo : c - lo + P], resid[:, c : c + P], ident[:])
+            nc.scalar.copy(flipped[:, lo:hi], flips[i][:, : hi - lo])
+        for i, lo in enumerate(range(0, VT, 512)):
+            for c in range(lo, lo + 512, P):
+                nc.tensor.transpose(backs[i][:, c - lo : c - lo + P], flipped[:, c : c + P], ident[:])
+        for lo in range(0, S, 512):
+            hi = lo + 512
+            nc.vector.tensor_tensor(routed[:].indirect(offsets[:, lo // 16 : hi // 16]), y[:, lo:hi], gates[:, lo:hi], MULT)
+        nc.gpsimd.tensor_tensor(total[:, V:T], routed[:, V:T], resid[:, V:T], ADD)
+        nc.sync.dma_start(out[:, V:T], total[:, V:T])
+        for i, lo in enumerate(range(0, V, 512)):
+            hi = min(lo + 512, V)
+            nc.vector.tensor_tensor(total[:, lo:hi], backs[i][:, : hi - lo], routed[:, lo:hi], ADD)
+            nc.sync.dma_start(out[:, lo:hi], total[:, lo:hi])

@@ -1,7 +1,6 @@
 from contextlib import ExitStack
 
 import concourse.mybir as mybir
-from concourse.masks import make_identity
 
 K, T, E, C, N = 1024, 1280, 8, 128, 128
 S = E * C
@@ -46,16 +45,14 @@ def tile_moe_res_lin_gelu_kernel(
         routed = held.tile([P, T], F32, name="routed")
         total = held.tile([P, T], F32, name="total")
         warm = held.tile([P, 8], F32, name="warm")
-        banks = [psum.tile([P, 512], F32, name=f"bank{e}") for e in range(4)]
-        NB = 4
+        banks = [psum.tile([P, 512], F32, name=f"bank{e}") for e in range(E)]
+        NB = E
 
         nc.gpsimd.memset(warm[:], 0.0)
         nc.gpsimd.memset(planes[:].bitcast(I32), 0)
         nc.gpsimd.memset(w8_plane[:].bitcast(I32), 0)
         nc.gpsimd.memset(w4_plane[:].bitcast(I32), 0)
         nc.gpsimd.memset(routed[:], 0.0)
-        ident = held.tile([P, P], F32, name="ident")
-        make_identity(nc, ident[:])
         nc.scalar.activation(warm[:], warm[:], GELU)
 
         x_view = xT.rearrange("(a p j) w -> a p j w", a=2, p=P, j=4)
@@ -64,7 +61,7 @@ def tile_moe_res_lin_gelu_kernel(
         w8_i = w8[:].bitcast(I32).rearrange("p (e n) -> p e n", e=E)
         w4_i = w4[:].bitcast(I32).rearrange("p (e n) -> p e n", e=E)
 
-        chunks = ((0, 0, 4, 0, 768), (0, 0, 4, 768, T), (1, 0, 4, 0, 512), (1, 0, 4, 512, 1024), (1, 0, 4, 1024, T))
+        chunks = ((0, 0, 4, 0, 512), (0, 0, 4, 512, 1024), (0, 0, 4, 1024, 1280), (1, 0, 4, 0, 256), (1, 0, 4, 256, 512), (1, 0, 4, 512, 768), (1, 0, 4, 768, 1024), (1, 0, 4, 1024, 1280))
         raw = []
         for i, (a, j, k, lo, hi) in enumerate(chunks):
             tile = held.tile([P, k - j, hi - lo], F32, name=f"raw{i}")
@@ -72,6 +69,7 @@ def tile_moe_res_lin_gelu_kernel(
             raw.append(tile)
             if i == 0:
                 nc.sync.dma_start(offsets[:], offs)
+                nc.sync.dma_start(bias[:], b)
 
         def load_scales(plane, scales):
             src = scales.rearrange("e a q n -> q (e a) n").bitcast(I32)
@@ -83,10 +81,9 @@ def tile_moe_res_lin_gelu_kernel(
             nc.sync.dma_start(w8_i[:, lo:hi, :], w8_view[:, lo:hi, :])
             nc.sync.dma_start(w4_i[:, lo:hi, :], w4_view[:, lo:hi, :])
 
+        load_words(0, 4)
         load_scales(w8_plane, w8_scales)
         load_scales(w4_plane, w4_scales)
-        nc.sync.dma_start(bias[:], b)
-        load_words(0, 4)
         nc.sync.dma_start(gates[:], gate)
         load_words(4, 8)
         nc.sync.dma_start(resid[:], xr)
@@ -102,7 +99,7 @@ def tile_moe_res_lin_gelu_kernel(
 
         def cast(grouped, src, vector):
             copy(
-                grouped[:].rearrange("p (w i) j -> p w j i", i=4), src.rearrange("p j (w i) -> p w j i", i=4), vector
+                grouped.rearrange("p (w i) j -> p w j i", i=4), src.rearrange("p j (w i) -> p w j i", i=4), vector
             )
 
         def quantise(grouped, a, lo, hi, base):
@@ -134,48 +131,30 @@ def tile_moe_res_lin_gelu_kernel(
                 stop=(a == 1),
             )
 
-        for i, (a, base, units) in enumerate((
-            (0, 0, ((512, 768, True), (0, 512, False))),
-            (0, 768, ((1024, 1280, True), (768, 1024, False))),
-            (1, 0, ((0, 512, False),)),
-            (1, 512, ((768, 1024, True), (512, 768, False))),
-            (1, 1024, ((1152, 1280, True), (1024, 1152, False))),
-        )):
-            for lo, hi, vector in units:
-                grouped = held.tile([P, hi - lo, 4], BF16, name=f"grouped{a}_{lo}", align_bytes=64)
-                cast(grouped, raw[i][:, :, lo - base : hi - base], vector)
-                quantise(grouped, a, lo, hi, lo)
-            if i == 1:
-                for lo in range(0, S, 512):
-                    gather(slot_codes[0], codes[0], lo, lo + 512)
+        scalar_share = (256, 256, 0, 256, 256, 256, 128, 128)
+        for i, (a, j, k, lo, hi) in enumerate(chunks):
+            grouped = held.tile([P, hi - lo, 4], BF16, name=f"grouped{i}", align_bytes=64)
+            cut = scalar_share[i]
+            if cut > 0:
+                cast(grouped[:, :cut, :], raw[i][:, :, :cut], False)
+            if cut < hi - lo:
+                cast(grouped[:, cut:, :], raw[i][:, :, cut:], True)
+            quantise(grouped, a, lo, hi, lo)
+            if a == 0 and hi == T:
+                for first in range(0, S, 512):
+                    gather(slot_codes[0], codes[0], first, first + 512)
 
         for lo in range(0, S, 512):
             gather(slot_planes, planes, lo, lo + 512)
             gather(slot_codes[1], codes[1], lo, lo + 512)
             for e in range(lo // C, (lo + 512) // C):
                 product(e, 0)
-            for e in range(lo // C, (lo + 512) // C):
                 product(e, 1)
                 nc.scalar.activation(y[:, e * C : (e + 1) * C], banks[e % NB][:, :C], GELU, bias=bias[:, e : e + 1])
-        V = 960
-        VT = 1024
-        flips = [psum.tile([P, 512], F32, name=f"flip{i}") for i in range(2)]
-        backs = [psum.tile([P, 512], F32, name=f"back{i}") for i in range(2)]
-        flipped = held.tile([P, VT], F32, name="flipped")
-        for i, lo in enumerate(range(0, VT, 512)):
-            hi = lo + 512
-            for c in range(lo, hi, P):
-                nc.tensor.transpose(flips[i][:, c - lo : c - lo + P], resid[:, c : c + P], ident[:])
-            nc.scalar.copy(flipped[:, lo:hi], flips[i][:, : hi - lo])
-        for i, lo in enumerate(range(0, VT, 512)):
-            for c in range(lo, lo + 512, P):
-                nc.tensor.transpose(backs[i][:, c - lo : c - lo + P], flipped[:, c : c + P], ident[:])
         for lo in range(0, S, 512):
             hi = lo + 512
             nc.vector.tensor_tensor(routed[:].indirect(offsets[:, lo // 16 : hi // 16]), y[:, lo:hi], gates[:, lo:hi], MULT)
-        nc.gpsimd.tensor_tensor(total[:, V:T], routed[:, V:T], resid[:, V:T], ADD)
-        nc.sync.dma_start(out[:, V:T], total[:, V:T])
-        for i, lo in enumerate(range(0, V, 512)):
-            hi = min(lo + 512, V)
-            nc.vector.tensor_tensor(total[:, lo:hi], backs[i][:, : hi - lo], routed[:, lo:hi], ADD)
+        for lo in range(0, T, 256):
+            hi = lo + 256
+            nc.vector.tensor_tensor(total[:, lo:hi], resid[:, lo:hi], routed[:, lo:hi], ADD)
             nc.sync.dma_start(out[:, lo:hi], total[:, lo:hi])

@@ -61,7 +61,7 @@ def tile_moe_res_lin_gelu_kernel(
         w8_i = w8[:].bitcast(I32).rearrange("p (e n) -> p e n", e=E)
         w4_i = w4[:].bitcast(I32).rearrange("p (e n) -> p e n", e=E)
 
-        chunks = ((0, 0, 4, 0, 512), (0, 0, 4, 512, 1024), (0, 0, 4, 1024, 1280), (1, 0, 4, 0, 256), (1, 0, 4, 256, 512), (1, 0, 4, 512, 768), (1, 0, 4, 768, 1024), (1, 0, 4, 1024, 1280))
+        chunks = ((0, 0, 4, 0, 768), (0, 0, 4, 768, 1280), (1, 0, 4, 0, 512), (1, 0, 4, 512, 1024), (1, 0, 4, 1024, 1280))
         raw = []
         for i, (a, j, k, lo, hi) in enumerate(chunks):
             tile = held.tile([P, k - j, hi - lo], F32, name=f"raw{i}")
@@ -131,15 +131,18 @@ def tile_moe_res_lin_gelu_kernel(
                 stop=(a == 1),
             )
 
-        scalar_share = (256, 256, 0, 256, 256, 256, 128, 128)
-        for i, (a, j, k, lo, hi) in enumerate(chunks):
-            grouped = held.tile([P, hi - lo, 4], BF16, name=f"grouped{i}", align_bytes=64)
-            cut = scalar_share[i]
-            if cut > 0:
-                cast(grouped[:, :cut, :], raw[i][:, :, :cut], False)
-            if cut < hi - lo:
-                cast(grouped[:, cut:, :], raw[i][:, :, cut:], True)
-            quantise(grouped, a, lo, hi, lo)
+        units = (
+            ((512, 768, True), (0, 512, False),),
+            ((1024, 1280, True), (768, 1024, False),),
+            ((0, 512, False),),
+            ((768, 1024, True), (512, 768, False),),
+            ((1152, 1280, True), (1024, 1152, False),),
+        )
+        for i, (a, j, k, base, hi) in enumerate(chunks):
+            for left, right, vector in units[i]:
+                grouped = held.tile([P, right - left, 4], BF16, name=f"grouped{a}_{left}", align_bytes=64)
+                cast(grouped[:], raw[i][:, :, left - base : right - base], vector)
+                quantise(grouped, a, left, right, left)
             if a == 0 and hi == T:
                 for first in range(0, S, 512):
                     gather(slot_codes[0], codes[0], first, first + 512)
@@ -154,7 +157,7 @@ def tile_moe_res_lin_gelu_kernel(
         for lo in range(0, S, 512):
             hi = lo + 512
             nc.vector.tensor_tensor(routed[:].indirect(offsets[:, lo // 16 : hi // 16]), y[:, lo:hi], gates[:, lo:hi], MULT)
-        for lo in range(0, T, 256):
-            hi = lo + 256
+        edges = (0, 320, 640, 960, 1280)
+        for lo, hi in zip(edges, edges[1:]):
             nc.vector.tensor_tensor(total[:, lo:hi], resid[:, lo:hi], routed[:, lo:hi], ADD)
             nc.sync.dma_start(out[:, lo:hi], total[:, lo:hi])

@@ -7,6 +7,7 @@ S = E * C
 FLOPS = 2 * S * K * N
 
 P = 128
+WINDOW = 1408
 F32 = mybir.dt.float32
 BF16 = mybir.dt.bfloat16
 I32 = mybir.dt.int32
@@ -30,8 +31,8 @@ def tile_moe_res_lin_gelu_kernel(
         psum = ctx.enter_context(tc.psum_pool(name="psum", bufs=1))
 
         offsets = held.tile([P, S // 16], U16, name="offsets")
-        codes = [held.tile([P, T], U32, name=f"codes{a}", align_bytes=64) for a in range(2)]
-        planes = held.tile([P, T], U8, name="planes", align_bytes=64)
+        codes = [held.tile([P, (WINDOW, T)[a]], U32, name=f"codes{a}", align_bytes=64) for a in range(2)]
+        planes = held.tile([P, WINDOW], U8, name="planes", align_bytes=64)
         slot_codes = [held.tile([P, S], U32, name=f"slot_codes{a}", align_bytes=64) for a in range(2)]
         slot_planes = held.tile([P, S], U8, name="slot_planes", align_bytes=64)
         w8 = held.tile([P, E * 512], U8, name="w8", align_bytes=64)
@@ -45,13 +46,14 @@ def tile_moe_res_lin_gelu_kernel(
         routed = held.tile([P, T], F32, name="routed")
         total = held.tile([P, T], F32, name="total")
         warm = held.tile([P, 8], F32, name="warm")
-        banks = [psum.tile([P, 512], F32, name=f"bank{e}") for e in range(E)]
-        NB = E
+        NB = 8
+        banks = [psum.tile([P, 512], F32, name=f"bank{e}") for e in range(NB)]
 
         nc.gpsimd.memset(warm[:], 0.0)
         nc.gpsimd.memset(planes[:].bitcast(I32), 0)
         nc.gpsimd.memset(w8_plane[:].bitcast(I32), 0)
         nc.gpsimd.memset(w4_plane[:].bitcast(I32), 0)
+        nc.gpsimd.memset(codes[0][:, T:WINDOW].bitcast(I32), 0)
         nc.gpsimd.memset(routed[:], 0.0)
         nc.scalar.activation(warm[:], warm[:], GELU)
 
@@ -61,15 +63,14 @@ def tile_moe_res_lin_gelu_kernel(
         w8_i = w8[:].bitcast(I32).rearrange("p (e n) -> p e n", e=E)
         w4_i = w4[:].bitcast(I32).rearrange("p (e n) -> p e n", e=E)
 
-        chunks = ((0, 0, 4, 0, 768), (0, 0, 4, 768, 1280), (1, 0, 4, 0, 512), (1, 0, 4, 512, 1024), (1, 0, 4, 1024, 1280))
+        chunks = ((0, 0, 768), (0, 768, 1280), (1, 0, 512), (1, 512, 1024), (1, 1024, 1280))
         raw = []
-        for i, (a, j, k, lo, hi) in enumerate(chunks):
-            tile = held.tile([P, k - j, hi - lo], F32, name=f"raw{i}")
-            nc.sync.dma_start(tile[:], x_view[a][:, j:k, lo:hi])
+        for i, (a, lo, hi) in enumerate(chunks):
+            tile = held.tile([P, 4, hi - lo], F32, name=f"raw{i}")
+            nc.sync.dma_start(tile[:], x_view[a][:, :, lo:hi])
             raw.append(tile)
-            if i == 0:
+            if i == 1:
                 nc.sync.dma_start(offsets[:], offs)
-                nc.sync.dma_start(bias[:], b)
 
         def load_scales(plane, scales):
             src = scales.rearrange("e a q n -> q (e a) n").bitcast(I32)
@@ -82,32 +83,27 @@ def tile_moe_res_lin_gelu_kernel(
             nc.sync.dma_start(w4_i[:, lo:hi, :], w4_view[:, lo:hi, :])
 
         load_words(0, 4)
+        nc.sync.dma_start(bias[:], b)
         load_scales(w8_plane, w8_scales)
         load_scales(w4_plane, w4_scales)
         nc.sync.dma_start(gates[:], gate)
         load_words(4, 8)
         nc.sync.dma_start(resid[:], xr)
 
-        def copy(dst, src, vector):
+        def cast(grouped, src, vector):
+            dst = grouped.rearrange("p (w i) j -> p w j i", i=4)
+            src = src.rearrange("p j (w i) -> p w j i", i=4)
             if vector:
                 nc.vector.tensor_copy(dst, src)
             else:
                 nc.scalar.activation(dst, src, COPY)
 
-        def cast_half(grouped, src, h, vector):
-            copy(grouped[:, :, 2 * h : 2 * h + 2], src.rearrange("p j w -> p w j"), vector)
-
-        def cast(grouped, src, vector):
-            copy(
-                grouped.rearrange("p (w i) j -> p w j i", i=4), src.rearrange("p j (w i) -> p w j i", i=4), vector
-            )
-
-        def quantise(grouped, a, lo, hi, base):
+        def quantise(grouped, a, lo, hi):
             first = 4 * (1 - a)
             nc.vector.quantize_mx(
                 codes[a][:, lo:hi].bitcast(FP8X4),
                 planes[first:P, lo:hi],
-                grouped[:, lo - base : hi - base, :].rearrange("p w j -> p (w j)"),
+                grouped.rearrange("p w j -> p (w j)"),
             )
 
         def gather(dst, src, lo, hi):
@@ -132,32 +128,37 @@ def tile_moe_res_lin_gelu_kernel(
             )
 
         units = (
-            ((512, 768, True), (0, 512, False),),
-            ((1024, 1280, True), (768, 1024, False),),
-            ((0, 512, False),),
-            ((768, 1024, True), (512, 768, False),),
-            ((1152, 1280, True), (1024, 1152, False),),
+            ((0, 512, 128), (512, 768, 256),),
+            ((1024, 1280, 0), (768, 1024, 256),),
+            ((0, 256, 256), (256, 512, 256),),
+            ((768, 1024, 0), (512, 768, 256),),
+            ((1024, 1280, 128),),
         )
-        for i, (a, j, k, base, hi) in enumerate(chunks):
-            for left, right, vector in units[i]:
-                grouped = held.tile([P, right - left, 4], BF16, name=f"grouped{a}_{left}", align_bytes=64)
-                cast(grouped[:], raw[i][:, :, left - base : right - base], vector)
-                quantise(grouped, a, left, right, left)
-            if a == 0 and hi == T:
-                for first in range(0, S, 512):
-                    gather(slot_codes[0], codes[0], first, first + 512)
+        for i, (a, base, end) in enumerate(chunks):
+            for lo, hi, cut in units[i]:
+                grouped = held.tile([P, hi - lo, 4], BF16, name=f"grouped{a}_{lo}", align_bytes=64)
+                src = raw[i][:, :, lo - base : hi - base]
+                if cut < hi - lo:
+                    cast(grouped[:, cut:, :], src[:, :, cut:], True)
+                if cut > 0:
+                    cast(grouped[:, :cut, :], src[:, :, :cut], False)
+                quantise(grouped[:], a, lo, hi)
+            if a == 0 and end == T:
+                for lo, hi in ((0, S),):
+                    gather(slot_codes[0], codes[0], lo, hi)
 
-        for lo in range(0, S, 512):
-            gather(slot_planes, planes, lo, lo + 512)
-            gather(slot_codes[1], codes[1], lo, lo + 512)
-            for e in range(lo // C, (lo + 512) // C):
+        groups = ((0, 512), (512, S))
+        for lo, hi in groups:
+            gather(slot_planes, planes, lo, hi)
+            gather(slot_codes[1], codes[1], lo, hi)
+            for e in range(lo // C, hi // C):
                 product(e, 0)
+            for e in range(lo // C, hi // C):
                 product(e, 1)
                 nc.scalar.activation(y[:, e * C : (e + 1) * C], banks[e % NB][:, :C], GELU, bias=bias[:, e : e + 1])
-        for lo in range(0, S, 512):
-            hi = lo + 512
+        for lo, hi in groups:
             nc.vector.tensor_tensor(routed[:].indirect(offsets[:, lo // 16 : hi // 16]), y[:, lo:hi], gates[:, lo:hi], MULT)
-        edges = (0, 320, 640, 960, 1280)
+        edges = (0, 256, 512, 768, 1024, 1280)
         for lo, hi in zip(edges, edges[1:]):
             nc.vector.tensor_tensor(total[:, lo:hi], resid[:, lo:hi], routed[:, lo:hi], ADD)
             nc.sync.dma_start(out[:, lo:hi], total[:, lo:hi])

@@ -49,10 +49,10 @@ def tile_moe_res_lin_gelu_kernel(
         NB = 8
         banks = [psum.tile([P, 512], F32, name=f"bank{e}") for e in range(NB)]
 
-        nc.gpsimd.memset(warm[:], 0.0)
-        nc.gpsimd.memset(planes[:].bitcast(I32), 0)
         nc.gpsimd.memset(w8_plane[:].bitcast(I32), 0)
+        nc.gpsimd.memset(warm[:], 0.0)
         nc.gpsimd.memset(w4_plane[:].bitcast(I32), 0)
+        nc.gpsimd.memset(planes[:].bitcast(I32), 0)
         nc.gpsimd.memset(codes[0][:, T:WINDOW].bitcast(I32), 0)
         nc.gpsimd.memset(routed[:], 0.0)
         nc.scalar.activation(warm[:], warm[:], GELU)
@@ -72,20 +72,21 @@ def tile_moe_res_lin_gelu_kernel(
             if i == 1:
                 nc.sync.dma_start(offsets[:], offs)
 
-        def load_scales(plane, scales):
+        def load_scales(plane, scales, rows):
             src = scales.rearrange("e a q n -> q (e a) n").bitcast(I32)
             dst = plane[:].bitcast(I32).rearrange("p (e n) -> p e n", e=E)
-            for quad in range(4):
-                nc.sync.dma_start(dst[32 * quad : 32 * quad + 4], src[4 * quad : 4 * quad + 4])
+            for r in rows:
+                nc.sync.dma_start(dst[r:P:32], src[r:16:4])
 
         def load_words(lo, hi):
             nc.sync.dma_start(w8_i[:, lo:hi, :], w8_view[:, lo:hi, :])
             nc.sync.dma_start(w4_i[:, lo:hi, :], w4_view[:, lo:hi, :])
 
+        load_scales(w8_plane, w8_scales, range(0, 2))
         load_words(0, 4)
+        load_scales(w8_plane, w8_scales, range(2, 4))
+        load_scales(w4_plane, w4_scales, range(0, 4))
         nc.sync.dma_start(bias[:], b)
-        load_scales(w8_plane, w8_scales)
-        load_scales(w4_plane, w4_scales)
         nc.sync.dma_start(gates[:], gate)
         load_words(4, 8)
         nc.sync.dma_start(resid[:], xr)

@@ -28,13 +28,12 @@ def tile_moe_res_lin_gelu_kernel(
     nc = tc.nc
     with ExitStack() as ctx:
         held = ctx.enter_context(tc.tile_pool(name="held", bufs=1))
+        reuse = ctx.enter_context(tc.tile_pool(name="reuse", bufs=1))
         psum = ctx.enter_context(tc.psum_pool(name="psum", bufs=1))
 
         offsets = held.tile([P, S // 16], U16, name="offsets")
-        codes = [held.tile([P, (WINDOW, T)[a]], U32, name=f"codes{a}", align_bytes=64) for a in range(2)]
-        planes = held.tile([P, WINDOW], U8, name="planes", align_bytes=64)
-        slot_codes = [held.tile([P, S], U32, name=f"slot_codes{a}", align_bytes=64) for a in range(2)]
-        slot_planes = held.tile([P, S], U8, name="slot_planes", align_bytes=64)
+        pairs = [held.tile([P, (WINDOW, WINDOW, WINDOW, T)[q]], U32, name=f"pairs{q}", align_bytes=64) for q in range(4)]
+        picked = [held.tile([P, 2, S], U32, name=f"picked{a}", align_bytes=64) for a in range(2)]
         w8 = held.tile([P, E * 512], U8, name="w8", align_bytes=64)
         w4 = held.tile([P, E * 256], U8, name="w4", align_bytes=64)
         w8_plane = held.tile([P, E * N], U8, name="w8_plane", align_bytes=64)
@@ -46,30 +45,38 @@ def tile_moe_res_lin_gelu_kernel(
         routed = held.tile([P, T], F32, name="routed")
         total = held.tile([P, T], F32, name="total")
         warm = held.tile([P, 8], F32, name="warm")
-        NB = 8
-        banks = [psum.tile([P, 512], F32, name=f"bank{e}") for e in range(NB)]
+        banks = [psum.tile([P, 512], F32, name=f"bank{e}") for e in range(E)]
 
-        nc.gpsimd.memset(w8_plane[:].bitcast(I32), 0)
         nc.gpsimd.memset(warm[:], 0.0)
+        for q in range(3):
+            nc.gpsimd.memset(pairs[q][:, T:WINDOW].bitcast(I32), 0)
+        nc.gpsimd.memset(w8_plane[:].bitcast(I32), 0)
         nc.gpsimd.memset(w4_plane[:].bitcast(I32), 0)
-        nc.gpsimd.memset(planes[:].bitcast(I32), 0)
-        nc.gpsimd.memset(codes[0][:, T:WINDOW].bitcast(I32), 0)
         nc.gpsimd.memset(routed[:], 0.0)
         nc.scalar.activation(warm[:], warm[:], GELU)
 
-        x_view = xT.rearrange("(a p j) w -> a p j w", a=2, p=P, j=4)
+        x_view = xT.rearrange("(a p u j) w -> a u p j w", a=2, p=P, u=2, j=2)
         w8_view = w8_words.rearrange("e a p n r -> p (e a) (n r)").bitcast(I32)
         w4_view = w4_words.rearrange("e a p n -> p (e a) n").bitcast(I32)
         w8_i = w8[:].bitcast(I32).rearrange("p (e n) -> p e n", e=E)
         w4_i = w4[:].bitcast(I32).rearrange("p (e n) -> p e n", e=E)
 
-        chunks = ((0, 0, 768), (0, 768, 1280), (1, 0, 512), (1, 512, 1024), (1, 1024, 1280))
+        chunks = (
+            (0, 0, 1280, (("vector", 832), ("scalar", 448))),
+            (1, 0, 1280, (("vector", 576), ("scalar", 704))),
+            (2, 0, 1280, (("gpsimd", 512), ("scalar", 768))),
+            (3, 0, 640, (("gpsimd", 512), ("scalar", 128))),
+            (3, 640, 1280, (("gpsimd", 224), ("scalar", 416))),
+        )
         raw = []
-        for i, (a, lo, hi) in enumerate(chunks):
-            tile = held.tile([P, 4, hi - lo], F32, name=f"raw{i}")
-            nc.sync.dma_start(tile[:], x_view[a][:, :, lo:hi])
+        for i, (q, lo, hi, shares) in enumerate(chunks):
+            if i == len(chunks) - 1:
+                tile = reuse.tile([P, 2, hi - lo], F32, name="raw_last", align_bytes=64, offset=0)
+            else:
+                tile = held.tile([P, 2, hi - lo], F32, name=f"raw{i}", align_bytes=64)
+            nc.sync.dma_start(tile[:], x_view[q // 2, q % 2][:, :, lo:hi])
             raw.append(tile)
-            if i == 1:
+            if i == 0:
                 nc.sync.dma_start(offsets[:], offs)
 
         def load_scales(plane, scales, rows):
@@ -91,27 +98,52 @@ def tile_moe_res_lin_gelu_kernel(
         load_words(4, 8)
         nc.sync.dma_start(resid[:], xr)
 
-        def cast(grouped, src, vector):
-            dst = grouped.rearrange("p (w i) j -> p w j i", i=4)
-            src = src.rearrange("p j (w i) -> p w j i", i=4)
+        def cast(i):
+            q, lo, hi, shares = chunks[i]
+            first = 0
+            for engine, width in shares:
+                last = first + width
+                dst = pairs[q][:, lo + first : lo + last].bitcast(BF16).rearrange("p (w j) -> p w j", j=2)
+                src = raw[i][:, :, first:last].rearrange("p j w -> p w j")
+                if engine == "vector":
+                    nc.vector.tensor_copy(dst, src)
+                elif engine == "scalar":
+                    nc.scalar.activation(dst, src, COPY)
+                else:
+                    nc.gpsimd.tensor_scalar(dst, src, 1.0, 0.0, MULT, ADD)
+                first = last
+            assert first == hi - lo
+
+        def gather(q, lo, hi):
+            nc.vector.tensor_copy(picked[q // 2][:, q % 2, lo:hi], pairs[q][:].indirect(offsets[:, lo // 16 : hi // 16]))
+
+        made = {}
+
+        def weave(a, lo, hi, vector, woven=None):
+            if woven is None:
+                woven = held.tile([P, hi - lo, 2], U32, name=f"woven{a}_{lo}", align_bytes=64)[:]
+            dst = woven
+            src = picked[a][:, :, lo:hi].rearrange("p u c -> p c u")
             if vector:
-                nc.vector.tensor_copy(dst, src)
+                nc.vector.tensor_copy(dst.bitcast(I32), src.bitcast(I32))
             else:
-                nc.scalar.activation(dst, src, COPY)
+                nc.scalar.copy(dst, src)
+            made[a, lo] = woven
 
-        def quantise(grouped, a, lo, hi):
-            first = 4 * (1 - a)
+        operand = {}
+
+        def quantise(a, lo, hi, plane=None, tag=None):
+            codes = held.tile([P, hi - lo], U32, name=f"codes{a}_{lo}", tag=tag or f"codes{a}_{lo}", align_bytes=64)
+            if plane is None:
+                plane = held.tile([P, hi - lo], U8, name=f"plane{a}_{lo}", align_bytes=64)
             nc.vector.quantize_mx(
-                codes[a][:, lo:hi].bitcast(FP8X4),
-                planes[first:P, lo:hi],
-                grouped.rearrange("p w j -> p (w j)"),
+                codes[:].bitcast(FP8X4), plane[:], made[a, lo].rearrange("p c u -> p (c u)").bitcast(BF16)
             )
-
-        def gather(dst, src, lo, hi):
-            nc.vector.tensor_copy(dst[:, lo:hi], src[:].indirect(offsets[:, lo // 16 : hi // 16]))
+            for e in range(lo // C, hi // C):
+                cols = slice(e * C - lo, (e + 1) * C - lo)
+                operand[a, e] = (codes[:, cols].bitcast(FP8X4), plane[:, cols])
 
         def product(e, a):
-            slots = slice(e * C, (e + 1) * C)
             if a == 0:
                 w = w8[:, 512 * e : 512 * (e + 1)].bitcast(FP8X4)
                 plane = w8_plane
@@ -119,46 +151,46 @@ def tile_moe_res_lin_gelu_kernel(
                 w = w4[:, 256 * e : 256 * (e + 1)].bitcast(FP4X4)
                 plane = w4_plane
             nc.tensor.matmul_mx(
-                out=banks[e % NB][:, :C],
+                out=banks[e][:, :C],
                 lhsT=w,
                 lhsT_scale=plane[:, e * N : (e + 1) * N],
-                rhs=slot_codes[a][:, slots].bitcast(FP8X4),
-                rhs_scale=slot_planes[4 * (1 - a) : P, slots],
+                rhs=operand[a, e][0],
+                rhs_scale=operand[a, e][1],
                 start=(a == 0),
                 stop=(a == 1),
             )
 
-        units = (
-            ((0, 512, 128), (512, 768, 256),),
-            ((1024, 1280, 0), (768, 1024, 256),),
-            ((0, 256, 256), (256, 512, 256),),
-            ((768, 1024, 0), (512, 768, 256),),
-            ((1024, 1280, 128),),
-        )
-        for i, (a, base, end) in enumerate(chunks):
-            for lo, hi, cut in units[i]:
-                grouped = held.tile([P, hi - lo, 4], BF16, name=f"grouped{a}_{lo}", align_bytes=64)
-                src = raw[i][:, :, lo - base : hi - base]
-                if cut < hi - lo:
-                    cast(grouped[:, cut:, :], src[:, :, cut:], True)
-                if cut > 0:
-                    cast(grouped[:, :cut, :], src[:, :, :cut], False)
-                quantise(grouped[:], a, lo, hi)
-            if a == 0 and end == T:
-                for lo, hi in ((0, S),):
-                    gather(slot_codes[0], codes[0], lo, hi)
-
-        groups = ((0, 512), (512, S))
-        for lo, hi in groups:
-            gather(slot_planes, planes, lo, hi)
-            gather(slot_codes[1], codes[1], lo, hi)
-            for e in range(lo // C, hi // C):
-                product(e, 0)
+        def finish(lo, hi):
             for e in range(lo // C, hi // C):
                 product(e, 1)
-                nc.scalar.activation(y[:, e * C : (e + 1) * C], banks[e % NB][:, :C], GELU, bias=bias[:, e : e + 1])
-        for lo, hi in groups:
+                nc.scalar.activation(y[:, e * C : (e + 1) * C], banks[e][:, :C], GELU, bias=bias[:, e : e + 1])
+
+        def scatter(lo, hi):
             nc.vector.tensor_tensor(routed[:].indirect(offsets[:, lo // 16 : hi // 16]), y[:, lo:hi], gates[:, lo:hi], MULT)
+
+        for q in range(3):
+            cast(q)
+            gather(q, 0, S)
+        first = held.tile([P, 512, 2], U32, name="first", tag="raw2", align_bytes=64)
+        weave(0, 0, 512, False, first[:])
+        cast(3)
+        cast(4)
+        second = reuse.tile([P, 512, 2], U32, name="second", align_bytes=64, offset=0)
+        weave(0, 512, S, False, second[:])
+        groups = ((0, 512), (512, S))
+        for lo, hi in groups:
+            gather(3, lo, hi)
+        for lo, hi in groups:
+            weave(1, lo, hi, False)
+        late = reuse.tile([P, 512], U8, name="late", align_bytes=64, offset=4096)
+        for lo, hi in groups:
+            quantise(0, lo, hi, late if lo == 0 else None, None if lo == 0 else "woven1_0")
+            quantise(1, lo, hi)
+            for e in range(lo // C, hi // C):
+                product(e, 0)
+            finish(lo, hi)
+        for lo, hi in ((0, 384), (384, S)):
+            scatter(lo, hi)
         edges = (0, 256, 512, 768, 1024, 1280)
         for lo, hi in zip(edges, edges[1:]):
             nc.vector.tensor_tensor(total[:, lo:hi], resid[:, lo:hi], routed[:, lo:hi], ADD)

@@ -32,7 +32,7 @@ def tile_moe_res_lin_gelu_kernel(
         psum = ctx.enter_context(tc.psum_pool(name="psum", bufs=1))
 
         offsets = held.tile([P, S // 16], U16, name="offsets")
-        pairs = [held.tile([P, (WINDOW, WINDOW, WINDOW, T)[q]], U32, name=f"pairs{q}", align_bytes=64) for q in range(4)]
+        pairs = [held.tile([P, (WINDOW, T, WINDOW, T)[q]], U32, name=f"pairs{q}", align_bytes=64) for q in range(4)]
         picked = [held.tile([P, 2, S], U32, name=f"picked{a}", align_bytes=64) for a in range(2)]
         w8 = held.tile([P, E * 512], U8, name="w8", align_bytes=64)
         w4 = held.tile([P, E * 256], U8, name="w4", align_bytes=64)
@@ -48,7 +48,7 @@ def tile_moe_res_lin_gelu_kernel(
         banks = [psum.tile([P, 512], F32, name=f"bank{e}") for e in range(E)]
 
         nc.gpsimd.memset(warm[:], 0.0)
-        for q in range(3):
+        for q in (0, 2):
             nc.gpsimd.memset(pairs[q][:, T:WINDOW].bitcast(I32), 0)
         nc.gpsimd.memset(w8_plane[:].bitcast(I32), 0)
         nc.gpsimd.memset(w4_plane[:].bitcast(I32), 0)
@@ -64,9 +64,10 @@ def tile_moe_res_lin_gelu_kernel(
         chunks = (
             (0, 0, 1280, (("vector", 832), ("scalar", 448))),
             (1, 0, 1280, (("vector", 576), ("scalar", 704))),
-            (2, 0, 1280, (("gpsimd", 512), ("scalar", 768))),
-            (3, 0, 640, (("gpsimd", 512), ("scalar", 128))),
-            (3, 640, 1280, (("gpsimd", 224), ("scalar", 416))),
+            (2, 0, 640, (("gpsimd", 288), ("scalar", 352))),
+            (2, 640, 1280, (("gpsimd", 256), ("scalar", 384))),
+            (3, 0, 640, (("gpsimd", 384), ("scalar", 256))),
+            (3, 640, 1280, (("gpsimd", 256), ("scalar", 384))),
         )
         raw = []
         for i, (q, lo, hi, shares) in enumerate(chunks):
@@ -168,13 +169,18 @@ def tile_moe_res_lin_gelu_kernel(
         def scatter(lo, hi):
             nc.vector.tensor_tensor(routed[:].indirect(offsets[:, lo // 16 : hi // 16]), y[:, lo:hi], gates[:, lo:hi], MULT)
 
-        for q in range(3):
-            cast(q)
-            gather(q, 0, S)
-        first = held.tile([P, 512, 2], U32, name="first", tag="raw2", align_bytes=64)
-        weave(0, 0, 512, False, first[:])
+        cast(0)
+        gather(0, 0, S)
+        cast(1)
+        gather(1, 0, 512)
+        gather(1, 512, S)
+        cast(2)
         cast(3)
+        gather(2, 0, S)
+        first = held.tile([P, 512, 2], U32, name="first", tag="raw3", align_bytes=64)
+        weave(0, 0, 512, False, first[:])
         cast(4)
+        cast(5)
         second = reuse.tile([P, 512, 2], U32, name="second", align_bytes=64, offset=0)
         weave(0, 512, S, False, second[:])
         groups = ((0, 512), (512, S))

@@ -8,6 +8,8 @@ FLOPS = 2 * S * K * N
 
 P = 128
 WINDOW = 1408
+RAW = 2 * T * 4
+HALF = S // 2
 F32 = mybir.dt.float32
 BF16 = mybir.dt.bfloat16
 I32 = mybir.dt.int32
@@ -32,8 +34,7 @@ def tile_moe_res_lin_gelu_kernel(
         psum = ctx.enter_context(tc.psum_pool(name="psum", bufs=1))
 
         offsets = held.tile([P, S // 16], U16, name="offsets")
-        pairs = [held.tile([P, (WINDOW, T, WINDOW, T)[q]], U32, name=f"pairs{q}", align_bytes=64) for q in range(4)]
-        picked = [held.tile([P, 2, S], U32, name=f"picked{a}", align_bytes=64) for a in range(2)]
+        pairs = [held.tile([P, (WINDOW, T, T, T)[q]], U32, name=f"pairs{q}", align_bytes=64) for q in range(4)]
         w8 = held.tile([P, E * 512], U8, name="w8", align_bytes=64)
         w4 = held.tile([P, E * 256], U8, name="w4", align_bytes=64)
         w8_plane = held.tile([P, E * N], U8, name="w8_plane", align_bytes=64)
@@ -47,9 +48,13 @@ def tile_moe_res_lin_gelu_kernel(
         warm = held.tile([P, 8], F32, name="warm")
         banks = [psum.tile([P, 512], F32, name=f"bank{e}") for e in range(E)]
 
+        def sums(e):
+            return banks[e][:, :C]
+
         nc.gpsimd.memset(warm[:], 0.0)
-        for q in (0, 2):
-            nc.gpsimd.memset(pairs[q][:, T:WINDOW].bitcast(I32), 0)
+        for q in range(4):
+            if (WINDOW, T, T, T)[q] > T:
+                nc.gpsimd.memset(pairs[q][:, T:WINDOW].bitcast(I32), 0)
         nc.gpsimd.memset(w8_plane[:].bitcast(I32), 0)
         nc.gpsimd.memset(w4_plane[:].bitcast(I32), 0)
         nc.gpsimd.memset(routed[:], 0.0)
@@ -62,23 +67,22 @@ def tile_moe_res_lin_gelu_kernel(
         w4_i = w4[:].bitcast(I32).rearrange("p (e n) -> p e n", e=E)
 
         chunks = (
-            (0, 0, 1280, (("vector", 832), ("scalar", 448))),
-            (1, 0, 1280, (("vector", 576), ("scalar", 704))),
-            (2, 0, 640, (("gpsimd", 288), ("scalar", 352))),
-            (2, 640, 1280, (("gpsimd", 256), ("scalar", 384))),
-            (3, 0, 640, (("gpsimd", 384), ("scalar", 256))),
-            (3, 640, 1280, (("gpsimd", 256), ("scalar", 384))),
+            (0, 0, 1280, (("vector", 832), ("scalar", 448),)),
+            (1, 0, 1280, (("vector", 576), ("scalar", 704),)),
+            (2, 0, 640, (("gpsimd", 288), ("scalar", 352),)),
+            (2, 640, 1280, (("gpsimd", 256), ("scalar", 384),)),
+            (3, 0, 640, (("gpsimd", 448), ("scalar", 192),)),
+            (3, 640, 1024, (("gpsimd", 160), ("scalar", 224),)),
+            (3, 1024, 1280, (("scalar", 256),)),
         )
         raw = []
         for i, (q, lo, hi, shares) in enumerate(chunks):
-            if i == len(chunks) - 1:
-                tile = reuse.tile([P, 2, hi - lo], F32, name="raw_last", align_bytes=64, offset=0)
-            else:
-                tile = held.tile([P, 2, hi - lo], F32, name=f"raw{i}", align_bytes=64)
+            tile = reuse.tile([P, 2, hi - lo], F32, name=f"raw{i}", align_bytes=64, offset=i * RAW)
             nc.sync.dma_start(tile[:], x_view[q // 2, q % 2][:, :, lo:hi])
             raw.append(tile)
             if i == 0:
                 nc.sync.dma_start(offsets[:], offs)
+        spare = len(chunks) * RAW
 
         def load_scales(plane, scales, rows):
             src = scales.rearrange("e a q n -> q (e a) n").bitcast(I32)
@@ -115,31 +119,26 @@ def tile_moe_res_lin_gelu_kernel(
                 first = last
             assert first == hi - lo
 
-        def gather(q, lo, hi):
-            nc.vector.tensor_copy(picked[q // 2][:, q % 2, lo:hi], pairs[q][:].indirect(offsets[:, lo // 16 : hi // 16]))
+        def gather(q, lo, hi, dst):
+            nc.vector.tensor_copy(dst, pairs[q][:].indirect(offsets[:, lo // 16 : hi // 16]))
 
-        made = {}
-
-        def weave(a, lo, hi, vector, woven=None):
-            if woven is None:
-                woven = held.tile([P, hi - lo, 2], U32, name=f"woven{a}_{lo}", align_bytes=64)[:]
-            dst = woven
-            src = picked[a][:, :, lo:hi].rearrange("p u c -> p c u")
-            if vector:
+        def weave(dst, src, engine="scalar"):
+            src = src.rearrange("p u c -> p c u")
+            if engine == "vector":
                 nc.vector.tensor_copy(dst.bitcast(I32), src.bitcast(I32))
+            elif engine == "gpsimd":
+                nc.gpsimd.tensor_copy(dst, src)
             else:
                 nc.scalar.copy(dst, src)
-            made[a, lo] = woven
 
         operand = {}
 
-        def quantise(a, lo, hi, plane=None, tag=None):
-            codes = held.tile([P, hi - lo], U32, name=f"codes{a}_{lo}", tag=tag or f"codes{a}_{lo}", align_bytes=64)
+        def quantise(a, lo, hi, woven, plane=None, codes=None):
+            if codes is None:
+                codes = held.tile([P, hi - lo], U32, name=f"codes{a}_{lo}", align_bytes=64)
             if plane is None:
                 plane = held.tile([P, hi - lo], U8, name=f"plane{a}_{lo}", align_bytes=64)
-            nc.vector.quantize_mx(
-                codes[:].bitcast(FP8X4), plane[:], made[a, lo].rearrange("p c u -> p (c u)").bitcast(BF16)
-            )
+            nc.vector.quantize_mx(codes[:].bitcast(FP8X4), plane[:], woven.rearrange("p c u -> p (c u)").bitcast(BF16))
             for e in range(lo // C, hi // C):
                 cols = slice(e * C - lo, (e + 1) * C - lo)
                 operand[a, e] = (codes[:, cols].bitcast(FP8X4), plane[:, cols])
@@ -152,7 +151,7 @@ def tile_moe_res_lin_gelu_kernel(
                 w = w4[:, 256 * e : 256 * (e + 1)].bitcast(FP4X4)
                 plane = w4_plane
             nc.tensor.matmul_mx(
-                out=banks[e][:, :C],
+                out=sums(e),
                 lhsT=w,
                 lhsT_scale=plane[:, e * N : (e + 1) * N],
                 rhs=operand[a, e][0],
@@ -164,37 +163,49 @@ def tile_moe_res_lin_gelu_kernel(
         def finish(lo, hi):
             for e in range(lo // C, hi // C):
                 product(e, 1)
-                nc.scalar.activation(y[:, e * C : (e + 1) * C], banks[e][:, :C], GELU, bias=bias[:, e : e + 1])
+                nc.scalar.activation(y[:, e * C : (e + 1) * C], sums(e), GELU, bias=bias[:, e : e + 1])
 
         def scatter(lo, hi):
             nc.vector.tensor_tensor(routed[:].indirect(offsets[:, lo // 16 : hi // 16]), y[:, lo:hi], gates[:, lo:hi], MULT)
 
+        picked0 = held.tile([P, 2, S], U32, name="picked0", align_bytes=64)
+        picked1 = [reuse.tile([P, 2, HALF], U32, name=f"picked1_{h}", align_bytes=64, offset=spare + h * 4096) for h in range(2)]
         cast(0)
-        gather(0, 0, S)
+        gather(0, 0, S, picked0[:, 0, :])
         cast(1)
-        gather(1, 0, 512)
-        gather(1, 512, S)
+        for h in range(2):
+            gather(1, h * HALF, (h + 1) * HALF, picked0[:, 1, h * HALF : (h + 1) * HALF])
         cast(2)
         cast(3)
-        gather(2, 0, S)
-        first = held.tile([P, 512, 2], U32, name="first", tag="raw3", align_bytes=64)
-        weave(0, 0, 512, False, first[:])
+        for h in range(2):
+            gather(2, h * HALF, (h + 1) * HALF, picked1[h][:, 0, :])
+        first = reuse.tile([P, HALF, 2], U32, name="first", align_bytes=64, offset=3 * RAW)
+        weave(first[:], picked0[:, :, :HALF])
         cast(4)
         cast(5)
-        second = reuse.tile([P, 512, 2], U32, name="second", align_bytes=64, offset=0)
-        weave(0, 512, S, False, second[:])
-        groups = ((0, 512), (512, S))
-        for lo, hi in groups:
-            gather(3, lo, hi)
-        for lo, hi in groups:
-            weave(1, lo, hi, False)
-        late = reuse.tile([P, 512], U8, name="late", align_bytes=64, offset=4096)
-        for lo, hi in groups:
-            quantise(0, lo, hi, late if lo == 0 else None, None if lo == 0 else "woven1_0")
-            quantise(1, lo, hi)
-            for e in range(lo // C, hi // C):
-                product(e, 0)
-            finish(lo, hi)
+        early = reuse.tile([P, HALF], U8, name="early", align_bytes=64, offset=5 * RAW)
+        quantise(0, 0, HALF, first[:], early)
+        cast(6)
+        second = reuse.tile([P, HALF, 2], U32, name="second", align_bytes=64, offset=6 * RAW)
+        woven = [held.tile([P, HALF, 2], U32, name=f"last{h}", align_bytes=64) for h in range(2)]
+        for part in range(4):
+            h, lo = part // 2, (part % 2) * 256
+            gather(3, part * 256, (part + 1) * 256, picked1[h][:, 1, lo : lo + 256])
+        weave(second[:], picked0[:, :, HALF:])
+        for part in range(4):
+            h, lo = part // 2, (part % 2) * 256
+            weave(woven[h][:, lo : lo + 256, :], picked1[h][:, :, lo : lo + 256])
+        quantise(1, 0, HALF, woven[0][:])
+        for e in range(0, 4):
+            product(e, 0)
+        finish(0, HALF)
+        late = reuse.tile([P, HALF], U8, name="late", align_bytes=64, offset=spare)
+        quantise(0, HALF, S, second[:], late)
+        quantise(1, HALF, S, woven[1][:])
+        for e in range(4, 8):
+            product(e, 0)
+        finish(HALF, S)
+
         for lo, hi in ((0, 384), (384, S)):
             scatter(lo, hi)
         edges = (0, 256, 512, 768, 1024, 1280)

@@ -10,6 +10,7 @@ P = 128
 WINDOW = 1408
 RAW = 2 * T * 4
 HALF = S // 2
+STAGGERED = (0, 1)
 F32 = mybir.dt.float32
 BF16 = mybir.dt.bfloat16
 I32 = mybir.dt.int32
@@ -61,26 +62,37 @@ def tile_moe_res_lin_gelu_kernel(
         nc.scalar.activation(warm[:], warm[:], GELU)
 
         x_view = xT.rearrange("(a p u j) w -> a u p j w", a=2, p=P, u=2, j=2)
+        x_flat = xT.rearrange("(a p u j) w -> a u p (j w)", a=2, p=P, u=2, j=2)
         w8_view = w8_words.rearrange("e a p n r -> p (e a) (n r)").bitcast(I32)
         w4_view = w4_words.rearrange("e a p n -> p (e a) n").bitcast(I32)
         w8_i = w8[:].bitcast(I32).rearrange("p (e n) -> p e n", e=E)
         w4_i = w4[:].bitcast(I32).rearrange("p (e n) -> p e n", e=E)
 
         chunks = (
-            (0, 0, 1280, (("vector", 832), ("scalar", 448),)),
-            (1, 0, 1280, (("vector", 576), ("scalar", 704),)),
-            (2, 0, 640, (("gpsimd", 288), ("scalar", 352),)),
-            (2, 640, 1280, (("gpsimd", 256), ("scalar", 384),)),
+            (0, 0, 704, (("vector", 448), ("scalar", 256),)),
+            (0, 704, 1280, (("vector", 384), ("scalar", 192),)),
+            (1, 0, 640, (("gpsimd", 256), ("scalar", 384),)),
+            (1, 640, 1280, (("gpsimd", 256), ("scalar", 384),)),
+            (2, 0, 768, (("gpsimd", 320), ("scalar", 448),)),
+            (2, 768, 1280, (("gpsimd", 192), ("scalar", 320),)),
             (3, 0, 640, (("gpsimd", 448), ("scalar", 192),)),
             (3, 640, 1024, (("gpsimd", 160), ("scalar", 224),)),
             (3, 1024, 1280, (("scalar", 256),)),
         )
         raw = []
+        flat = {}
         for i, (q, lo, hi, shares) in enumerate(chunks):
-            tile = reuse.tile([P, 2, hi - lo], F32, name=f"raw{i}", align_bytes=64, offset=i * RAW)
-            nc.sync.dma_start(tile[:], x_view[q // 2, q % 2][:, :, lo:hi])
-            raw.append(tile)
-            if i == 0:
+            if q in STAGGERED:
+                if lo == 0:
+                    flat[q] = reuse.tile([P, 2 * T], F32, name=f"raw{i}", align_bytes=64, offset=i * RAW)
+                begin = 0 if lo == 0 else T + lo
+                nc.sync.dma_start(flat[q][:, begin : T + hi], x_flat[q // 2, q % 2][:, begin : T + hi])
+                raw.append(flat[q][:].rearrange("p (j w) -> p j w", j=2)[:, :, lo:hi])
+            else:
+                tile = reuse.tile([P, 2, hi - lo], F32, name=f"raw{i}", align_bytes=64, offset=i * RAW)
+                nc.sync.dma_start(tile[:], x_view[q // 2, q % 2][:, :, lo:hi])
+                raw.append(tile[:])
+            if i == 1:
                 nc.sync.dma_start(offsets[:], offs)
         spare = len(chunks) * RAW
 
@@ -171,22 +183,24 @@ def tile_moe_res_lin_gelu_kernel(
         picked0 = held.tile([P, 2, S], U32, name="picked0", align_bytes=64)
         picked1 = [reuse.tile([P, 2, HALF], U32, name=f"picked1_{h}", align_bytes=64, offset=spare + h * 4096) for h in range(2)]
         cast(0)
-        gather(0, 0, S, picked0[:, 0, :])
         cast(1)
-        for h in range(2):
-            gather(1, h * HALF, (h + 1) * HALF, picked0[:, 1, h * HALF : (h + 1) * HALF])
+        gather(0, 0, S, picked0[:, 0, :])
         cast(2)
         cast(3)
         for h in range(2):
-            gather(2, h * HALF, (h + 1) * HALF, picked1[h][:, 0, :])
-        first = reuse.tile([P, HALF, 2], U32, name="first", align_bytes=64, offset=3 * RAW)
-        weave(first[:], picked0[:, :, :HALF])
+            gather(1, h * HALF, (h + 1) * HALF, picked0[:, 1, h * HALF : (h + 1) * HALF])
         cast(4)
         cast(5)
-        early = reuse.tile([P, HALF], U8, name="early", align_bytes=64, offset=5 * RAW)
-        quantise(0, 0, HALF, first[:], early)
+        for h in range(2):
+            gather(2, h * HALF, (h + 1) * HALF, picked1[h][:, 0, :])
+        first = reuse.tile([P, HALF, 2], U32, name="first", align_bytes=64, offset=5 * RAW)
+        weave(first[:], picked0[:, :, :HALF])
         cast(6)
-        second = reuse.tile([P, HALF, 2], U32, name="second", align_bytes=64, offset=6 * RAW)
+        cast(7)
+        early = reuse.tile([P, HALF], U8, name="early", align_bytes=64, offset=7 * RAW)
+        quantise(0, 0, HALF, first[:], early)
+        cast(8)
+        second = reuse.tile([P, HALF, 2], U32, name="second", align_bytes=64, offset=8 * RAW)
         woven = [held.tile([P, HALF, 2], U32, name=f"last{h}", align_bytes=64) for h in range(2)]
         for part in range(4):
             h, lo = part // 2, (part % 2) * 256

@@ -111,8 +111,9 @@ def tile_moe_res_lin_gelu_kernel(
         load_scales(w8_plane, w8_scales, range(2, 4))
         load_scales(w4_plane, w4_scales, range(0, 4))
         nc.sync.dma_start(bias[:], b)
-        nc.sync.dma_start(gates[:], gate)
+        nc.sync.dma_start(gates[:, :384], gate[:, :384])
         load_words(4, 8)
+        nc.sync.dma_start(gates[:, 384:], gate[:, 384:])
         nc.sync.dma_start(resid[:], xr)
 
         def cast(i):
@@ -209,10 +210,11 @@ def tile_moe_res_lin_gelu_kernel(
         for part in range(4):
             h, lo = part // 2, (part % 2) * 256
             weave(woven[h][:, lo : lo + 256, :], picked1[h][:, :, lo : lo + 256])
-        quantise(1, 0, HALF, woven[0][:])
         for e in range(0, 4):
             product(e, 0)
-        finish(0, HALF)
+        for lo in (0, 256):
+            quantise(1, lo, lo + 256, woven[0][:, lo : lo + 256, :])
+            finish(lo, lo + 256)
         late = reuse.tile([P, HALF], U8, name="late", align_bytes=64, offset=spare)
         quantise(0, HALF, S, second[:], late)
         quantise(1, HALF, S, woven[1][:])

@@ -123,6 +123,9 @@ def tile_moe_res_lin_gelu_kernel(
                 last = first + width
                 dst = pairs[q][:, lo + first : lo + last].bitcast(BF16).rearrange("p (w j) -> p w j", j=2)
                 src = raw[i][:, :, first:last].rearrange("p j w -> p w j")
+                if engine != "gpsimd":
+                    dst = dst.rearrange("p (c i) j -> p c j i", i=4)
+                    src = src.rearrange("p (c i) j -> p c j i", i=4)
                 if engine == "vector":
                     nc.vector.tensor_copy(dst, src)
                 elif engine == "scalar":
@@ -136,7 +139,8 @@ def tile_moe_res_lin_gelu_kernel(
             nc.vector.tensor_copy(dst, pairs[q][:].indirect(offsets[:, lo // 16 : hi // 16]))
 
         def weave(dst, src, engine="scalar"):
-            src = src.rearrange("p u c -> p c u")
+            src = src.rearrange("p u (c i) -> p c u i", i=2)
+            dst = dst.rearrange("p (c i) u -> p c u i", i=2)
             if engine == "vector":
                 nc.vector.tensor_copy(dst.bitcast(I32), src.bitcast(I32))
             elif engine == "gpsimd":

@@ -72,11 +72,11 @@ def tile_moe_res_lin_gelu_kernel(
             (0, 0, 704, (("vector", 448), ("scalar", 256),)),
             (0, 704, 1280, (("vector", 384), ("scalar", 192),)),
             (1, 0, 640, (("gpsimd", 256), ("scalar", 384),)),
-            (1, 640, 1280, (("gpsimd", 256), ("scalar", 384),)),
-            (2, 0, 768, (("gpsimd", 320), ("scalar", 448),)),
+            (1, 640, 1280, (("scalar", 320), ("vector", 320),)),
+            (2, 0, 768, (("gpsimd", 224), ("scalar", 544),)),
             (2, 768, 1280, (("gpsimd", 192), ("scalar", 320),)),
-            (3, 0, 640, (("gpsimd", 448), ("scalar", 192),)),
-            (3, 640, 1024, (("gpsimd", 160), ("scalar", 224),)),
+            (3, 0, 576, (("gpsimd", 576),)),
+            (3, 576, 1024, (("scalar", 448),)),
             (3, 1024, 1280, (("scalar", 256),)),
         )
         raw = []
@@ -139,8 +139,11 @@ def tile_moe_res_lin_gelu_kernel(
             nc.vector.tensor_copy(dst, pairs[q][:].indirect(offsets[:, lo // 16 : hi // 16]))
 
         def weave(dst, src, engine="scalar"):
-            src = src.rearrange("p u (c i) -> p c u i", i=2)
-            dst = dst.rearrange("p (c i) u -> p c u i", i=2)
+            if engine == "gpsimd":
+                src = src.rearrange("p u c -> p c u")
+            else:
+                src = src.rearrange("p u (c i) -> p c u i", i=2)
+                dst = dst.rearrange("p (c i) u -> p c u i", i=2)
             if engine == "vector":
                 nc.vector.tensor_copy(dst.bitcast(I32), src.bitcast(I32))
             elif engine == "gpsimd":
@@ -198,22 +201,22 @@ def tile_moe_res_lin_gelu_kernel(
         cast(5)
         for h in range(2):
             gather(2, h * HALF, (h + 1) * HALF, picked1[h][:, 0, :])
-        first = reuse.tile([P, HALF, 2], U32, name="first", align_bytes=64, offset=5 * RAW)
-        weave(first[:], picked0[:, :, :HALF])
+        first = reuse.tile([P, HALF, 2], U32, name="first", align_bytes=64, offset=4 * RAW)
+        weave(first[:], picked0[:, :, :HALF], "scalar")
         cast(6)
         cast(7)
-        early = reuse.tile([P, HALF], U8, name="early", align_bytes=64, offset=7 * RAW)
+        early = reuse.tile([P, HALF], U8, name="early", align_bytes=64, offset=6 * RAW)
         quantise(0, 0, HALF, first[:], early)
         cast(8)
-        second = reuse.tile([P, HALF, 2], U32, name="second", align_bytes=64, offset=8 * RAW)
+        second = reuse.tile([P, HALF, 2], U32, name="second", align_bytes=64, offset=4 * RAW)
         woven = [held.tile([P, HALF, 2], U32, name=f"last{h}", align_bytes=64) for h in range(2)]
-        for part in range(4):
-            h, lo = part // 2, (part % 2) * 256
-            gather(3, part * 256, (part + 1) * 256, picked1[h][:, 1, lo : lo + 256])
-        weave(second[:], picked0[:, :, HALF:])
-        for part in range(4):
-            h, lo = part // 2, (part % 2) * 256
-            weave(woven[h][:, lo : lo + 256, :], picked1[h][:, :, lo : lo + 256])
+        parts = (0, 256, 512, 832, 1024)
+        for lo, hi in zip(parts, parts[1:]):
+            gather(3, lo, hi, picked1[lo // HALF][:, 1, lo % HALF : lo % HALF + hi - lo])
+        weave(second[:], picked0[:, :, HALF:], "gpsimd")
+        for lo, hi in zip(parts, parts[1:]):
+            cols = slice(lo % HALF, lo % HALF + hi - lo)
+            weave(woven[lo // HALF][:, cols, :], picked1[lo // HALF][:, :, cols])
         for e in range(0, 4):
             product(e, 0)
         for lo in (0, 256):

@@ -44,7 +44,7 @@ def tile_moe_res_lin_gelu_kernel(
         gates = held.tile([P, S], F32, name="gates")
         resid = held.tile([P, T], F32, name="resid")
         y = held.tile([P, S], F32, name="y")
-        routed = held.tile([P, T], F32, name="routed")
+        routed = held.tile([P, 1536], F32, name="routed")
         total = held.tile([P, T], F32, name="total")
         warm = held.tile([P, 8], F32, name="warm")
         banks = [psum.tile([P, 512], F32, name=f"bank{e}") for e in range(E)]
@@ -58,7 +58,7 @@ def tile_moe_res_lin_gelu_kernel(
                 nc.gpsimd.memset(pairs[q][:, T:WINDOW].bitcast(I32), 0)
         nc.gpsimd.memset(w8_plane[:].bitcast(I32), 0)
         nc.gpsimd.memset(w4_plane[:].bitcast(I32), 0)
-        nc.gpsimd.memset(routed[:], 0.0)
+        nc.gpsimd.memset(routed[:, :T], 0.0)
         nc.scalar.activation(warm[:], warm[:], GELU)
 
         x_view = xT.rearrange("(a p u j) w -> a u p j w", a=2, p=P, u=2, j=2)
@@ -111,9 +111,9 @@ def tile_moe_res_lin_gelu_kernel(
         load_scales(w8_plane, w8_scales, range(2, 4))
         load_scales(w4_plane, w4_scales, range(0, 4))
         nc.sync.dma_start(bias[:], b)
-        nc.sync.dma_start(gates[:, :384], gate[:, :384])
+        nc.sync.dma_start(gates[:, :256], gate[:, :256])
         load_words(4, 8)
-        nc.sync.dma_start(gates[:, 384:], gate[:, 384:])
+        nc.sync.dma_start(gates[:, 256:], gate[:, 256:])
         nc.sync.dma_start(resid[:], xr)
 
         def cast(i):
@@ -140,14 +140,15 @@ def tile_moe_res_lin_gelu_kernel(
 
         def weave(dst, src, engine="scalar"):
             if engine == "gpsimd":
-                src = src.rearrange("p u c -> p c u")
+                src = src.bitcast(BF16).rearrange("p u (c j) -> p c u j", j=2)
+                dst = dst.bitcast(BF16).rearrange("p c (u j) -> p c u j", j=2)
             else:
                 src = src.rearrange("p u (c i) -> p c u i", i=2)
                 dst = dst.rearrange("p (c i) u -> p c u i", i=2)
             if engine == "vector":
                 nc.vector.tensor_copy(dst.bitcast(I32), src.bitcast(I32))
             elif engine == "gpsimd":
-                nc.gpsimd.tensor_copy(dst, src)
+                nc.gpsimd.tensor_scalar(dst, src, 1.0, 0.0, MULT, ADD)
             else:
                 nc.scalar.copy(dst, src)
 
@@ -210,13 +211,14 @@ def tile_moe_res_lin_gelu_kernel(
         cast(8)
         second = reuse.tile([P, HALF, 2], U32, name="second", align_bytes=64, offset=4 * RAW)
         woven = [held.tile([P, HALF, 2], U32, name=f"last{h}", align_bytes=64) for h in range(2)]
-        parts = (0, 256, 512, 832, 1024)
-        for lo, hi in zip(parts, parts[1:]):
-            gather(3, lo, hi, picked1[lo // HALF][:, 1, lo % HALF : lo % HALF + hi - lo])
-        weave(second[:], picked0[:, :, HALF:], "gpsimd")
-        for lo, hi in zip(parts, parts[1:]):
-            cols = slice(lo % HALF, lo % HALF + hi - lo)
-            weave(woven[lo // HALF][:, cols, :], picked1[lo // HALF][:, :, cols])
+        for part in range(4):
+            h, lo = part // 2, (part % 2) * 256
+            gather(3, part * 256, (part + 1) * 256, picked1[h][:, 1, lo : lo + 256])
+        weave(second[:, :256, :], picked0[:, :, HALF:768], "scalar")
+        weave(second[:, 256:, :], picked0[:, :, 768:], "gpsimd")
+        for part in range(4):
+            h, lo = part // 2, (part % 2) * 256
+            weave(woven[h][:, lo : lo + 256, :], picked1[h][:, :, lo : lo + 256])
         for e in range(0, 4):
             product(e, 0)
         for lo in (0, 256):
@@ -224,12 +226,13 @@ def tile_moe_res_lin_gelu_kernel(
             finish(lo, lo + 256)
         late = reuse.tile([P, HALF], U8, name="late", align_bytes=64, offset=spare)
         quantise(0, HALF, S, second[:], late)
-        quantise(1, HALF, S, woven[1][:])
         for e in range(4, 8):
             product(e, 0)
-        finish(HALF, S)
+        for lo in (0, 256):
+            quantise(1, HALF + lo, HALF + lo + 256, woven[1][:, lo : lo + 256, :])
+            finish(HALF + lo, HALF + lo + 256)
 
-        for lo, hi in ((0, 384), (384, S)):
+        for lo, hi in ((0, 256), (256, S)):
             scatter(lo, hi)
         edges = (0, 256, 512, 768, 1024, 1280)
         for lo, hi in zip(edges, edges[1:]):

@@ -7,10 +7,23 @@ S = E * C
 FLOPS = 2 * S * K * N
 
 P = 128
-WINDOW = 1408
-RAW = 2 * T * 4
 HALF = S // 2
+QUARTER = S // 4
+GATHER_WINDOW = 1408
+SCATTER_WINDOW = 1536
+RAW = 2 * T * 4
+STORE = 256
+
 STAGGERED = (0, 1)
+CUTS = ((704,), (640,), (512, 960), (512, 960))
+SHARES = (
+    (("vector", 2 / 3), ("vector", 2 / 3)),
+    (("gpsimd", 1 / 2), ("vector", 4 / 9)),
+    (("gpsimd", 3 / 7), ("gpsimd", 3 / 7), ("gpsimd", 3 / 7)),
+    (("gpsimd", 1 / 2), ("gpsimd", 1 / 2), ("gpsimd", 0)),
+)
+SHARE_STEP = 32
+
 F32 = mybir.dt.float32
 BF16 = mybir.dt.bfloat16
 I32 = mybir.dt.int32
@@ -35,7 +48,7 @@ def tile_moe_res_lin_gelu_kernel(
         psum = ctx.enter_context(tc.psum_pool(name="psum", bufs=1))
 
         offsets = held.tile([P, S // 16], U16, name="offsets")
-        pairs = [held.tile([P, (WINDOW, T, T, T)[q]], U32, name=f"pairs{q}", align_bytes=64) for q in range(4)]
+        pairs = [held.tile([P, GATHER_WINDOW if q == 0 else T], U32, name=f"pairs{q}", align_bytes=64) for q in range(4)]
         w8 = held.tile([P, E * 512], U8, name="w8", align_bytes=64)
         w4 = held.tile([P, E * 256], U8, name="w4", align_bytes=64)
         w8_plane = held.tile([P, E * N], U8, name="w8_plane", align_bytes=64)
@@ -44,57 +57,45 @@ def tile_moe_res_lin_gelu_kernel(
         gates = held.tile([P, S], F32, name="gates")
         resid = held.tile([P, T], F32, name="resid")
         y = held.tile([P, S], F32, name="y")
-        routed = held.tile([P, 1536], F32, name="routed")
+        routed = held.tile([P, SCATTER_WINDOW], F32, name="routed")
         total = held.tile([P, T], F32, name="total")
         warm = held.tile([P, 8], F32, name="warm")
         banks = [psum.tile([P, 512], F32, name=f"bank{e}") for e in range(E)]
 
-        def sums(e):
-            return banks[e][:, :C]
-
         nc.gpsimd.memset(warm[:], 0.0)
-        for q in range(4):
-            if (WINDOW, T, T, T)[q] > T:
-                nc.gpsimd.memset(pairs[q][:, T:WINDOW].bitcast(I32), 0)
+        nc.gpsimd.memset(pairs[0][:, T:].bitcast(I32), 0)
         nc.gpsimd.memset(w8_plane[:].bitcast(I32), 0)
         nc.gpsimd.memset(w4_plane[:].bitcast(I32), 0)
         nc.gpsimd.memset(routed[:, :T], 0.0)
         nc.scalar.activation(warm[:], warm[:], GELU)
 
-        x_view = xT.rearrange("(a p u j) w -> a u p j w", a=2, p=P, u=2, j=2)
-        x_flat = xT.rearrange("(a p u j) w -> a u p (j w)", a=2, p=P, u=2, j=2)
+        x_columns = xT.rearrange("(a p u j) w -> a u p j w", a=2, p=P, u=2, j=2)
+        x_runs = xT.rearrange("(a p u j) w -> a u p (j w)", a=2, p=P, u=2, j=2)
         w8_view = w8_words.rearrange("e a p n r -> p (e a) (n r)").bitcast(I32)
         w4_view = w4_words.rearrange("e a p n -> p (e a) n").bitcast(I32)
         w8_i = w8[:].bitcast(I32).rearrange("p (e n) -> p e n", e=E)
         w4_i = w4[:].bitcast(I32).rearrange("p (e n) -> p e n", e=E)
 
-        chunks = (
-            (0, 0, 704, (("vector", 448), ("scalar", 256),)),
-            (0, 704, 1280, (("vector", 384), ("scalar", 192),)),
-            (1, 0, 640, (("gpsimd", 256), ("scalar", 384),)),
-            (1, 640, 1280, (("scalar", 320), ("vector", 320),)),
-            (2, 0, 768, (("gpsimd", 224), ("scalar", 544),)),
-            (2, 768, 1280, (("gpsimd", 192), ("scalar", 320),)),
-            (3, 0, 576, (("gpsimd", 576),)),
-            (3, 576, 1024, (("scalar", 448),)),
-            (3, 1024, 1280, (("scalar", 256),)),
-        )
-        raw = []
-        flat = {}
-        for i, (q, lo, hi, shares) in enumerate(chunks):
-            if q in STAGGERED:
-                if lo == 0:
-                    flat[q] = reuse.tile([P, 2 * T], F32, name=f"raw{i}", align_bytes=64, offset=i * RAW)
-                begin = 0 if lo == 0 else T + lo
-                nc.sync.dma_start(flat[q][:, begin : T + hi], x_flat[q // 2, q % 2][:, begin : T + hi])
-                raw.append(flat[q][:].rearrange("p (j w) -> p j w", j=2)[:, :, lo:hi])
-            else:
-                tile = reuse.tile([P, 2, hi - lo], F32, name=f"raw{i}", align_bytes=64, offset=i * RAW)
-                nc.sync.dma_start(tile[:], x_view[q // 2, q % 2][:, :, lo:hi])
-                raw.append(tile[:])
-            if i == 1:
+        edges = [(0, *cuts, T) for cuts in CUTS]
+        raw = [[] for q in range(4)]
+        raw_at = [[] for q in range(4)]
+        spare = 0
+        for q in range(4):
+            for lo, hi in zip(edges[q], edges[q][1:]):
+                if q in STAGGERED:
+                    if lo == 0:
+                        run = reuse.tile([P, 2 * T], F32, name=f"raw{q}", align_bytes=64, offset=spare)
+                    begin = 0 if lo == 0 else T + lo
+                    nc.sync.dma_start(run[:, begin : T + hi], x_runs[q // 2, q % 2][:, begin : T + hi])
+                    raw[q].append(run[:].rearrange("p (j w) -> p j w", j=2)[:, :, lo:hi])
+                else:
+                    piece = reuse.tile([P, 2, hi - lo], F32, name=f"raw{q}_{lo}", align_bytes=64, offset=spare)
+                    nc.sync.dma_start(piece[:], x_columns[q // 2, q % 2][:, :, lo:hi])
+                    raw[q].append(piece[:])
+                raw_at[q].append(spare)
+                spare += RAW
+            if q == 0:
                 nc.sync.dma_start(offsets[:], offs)
-        spare = len(chunks) * RAW
 
         def load_scales(plane, scales, rows):
             src = scales.rearrange("e a q n -> q (e a) n").bitcast(I32)
@@ -107,56 +108,58 @@ def tile_moe_res_lin_gelu_kernel(
             nc.sync.dma_start(w4_i[:, lo:hi, :], w4_view[:, lo:hi, :])
 
         load_scales(w8_plane, w8_scales, range(0, 2))
-        load_words(0, 4)
+        load_words(0, E // 2)
         load_scales(w8_plane, w8_scales, range(2, 4))
         load_scales(w4_plane, w4_scales, range(0, 4))
         nc.sync.dma_start(bias[:], b)
-        nc.sync.dma_start(gates[:, :256], gate[:, :256])
-        load_words(4, 8)
-        nc.sync.dma_start(gates[:, 256:], gate[:, 256:])
+        nc.sync.dma_start(gates[:, :QUARTER], gate[:, :QUARTER])
+        load_words(E // 2, E)
+        nc.sync.dma_start(gates[:, QUARTER:], gate[:, QUARTER:])
         nc.sync.dma_start(resid[:], xr)
 
-        def cast(i):
-            q, lo, hi, shares = chunks[i]
-            first = 0
-            for engine, width in shares:
-                last = first + width
+        def round_load(q, i):
+            lo, hi = edges[q][i], edges[q][i + 1]
+            helper, share = SHARES[q][i]
+            cut = round((hi - lo) * share / SHARE_STEP) * SHARE_STEP
+            for engine, first, last in ((helper, 0, cut), ("scalar", cut, hi - lo)):
+                if first == last:
+                    continue
                 dst = pairs[q][:, lo + first : lo + last].bitcast(BF16).rearrange("p (w j) -> p w j", j=2)
-                src = raw[i][:, :, first:last].rearrange("p j w -> p w j")
-                if engine != "gpsimd":
-                    dst = dst.rearrange("p (c i) j -> p c j i", i=4)
-                    src = src.rearrange("p (c i) j -> p c j i", i=4)
+                src = raw[q][i][:, :, first:last].rearrange("p j w -> p w j")
+                if engine == "gpsimd":
+                    nc.gpsimd.tensor_scalar(dst, src, 1.0, 0.0, MULT, ADD)
+                    continue
+                dst = dst.rearrange("p (c i) j -> p c j i", i=4)
+                src = src.rearrange("p (c i) j -> p c j i", i=4)
                 if engine == "vector":
                     nc.vector.tensor_copy(dst, src)
-                elif engine == "scalar":
-                    nc.scalar.activation(dst, src, COPY)
                 else:
-                    nc.gpsimd.tensor_scalar(dst, src, 1.0, 0.0, MULT, ADD)
-                first = last
-            assert first == hi - lo
+                    nc.scalar.activation(dst, src, COPY)
+
+        def round_pair(q):
+            for i in range(len(raw[q])):
+                round_load(q, i)
 
         def gather(q, lo, hi, dst):
             nc.vector.tensor_copy(dst, pairs[q][:].indirect(offsets[:, lo // 16 : hi // 16]))
 
-        def weave(dst, src, engine="scalar"):
-            if engine == "gpsimd":
-                src = src.bitcast(BF16).rearrange("p u (c j) -> p c u j", j=2)
-                dst = dst.bitcast(BF16).rearrange("p c (u j) -> p c u j", j=2)
-            else:
-                src = src.rearrange("p u (c i) -> p c u i", i=2)
-                dst = dst.rearrange("p (c i) u -> p c u i", i=2)
-            if engine == "vector":
-                nc.vector.tensor_copy(dst.bitcast(I32), src.bitcast(I32))
-            elif engine == "gpsimd":
-                nc.gpsimd.tensor_scalar(dst, src, 1.0, 0.0, MULT, ADD)
-            else:
-                nc.scalar.copy(dst, src)
+        def weave_on_scalar(dst, src):
+            nc.scalar.copy(dst.rearrange("p (c i) u -> p c u i", i=2), src.rearrange("p u (c i) -> p c u i", i=2))
+
+        def weave_on_gpsimd(dst, src):
+            nc.gpsimd.tensor_scalar(
+                dst.bitcast(BF16).rearrange("p c (u j) -> p c u j", j=2),
+                src.bitcast(BF16).rearrange("p u (c j) -> p c u j", j=2),
+                1.0,
+                0.0,
+                MULT,
+                ADD,
+            )
 
         operand = {}
 
-        def quantise(a, lo, hi, woven, plane=None, codes=None):
-            if codes is None:
-                codes = held.tile([P, hi - lo], U32, name=f"codes{a}_{lo}", align_bytes=64)
+        def quantise(a, lo, hi, woven, plane=None):
+            codes = held.tile([P, hi - lo], U32, name=f"codes{a}_{lo}", align_bytes=64)
             if plane is None:
                 plane = held.tile([P, hi - lo], U8, name=f"plane{a}_{lo}", align_bytes=64)
             nc.vector.quantize_mx(codes[:].bitcast(FP8X4), plane[:], woven.rearrange("p c u -> p (c u)").bitcast(BF16))
@@ -164,77 +167,73 @@ def tile_moe_res_lin_gelu_kernel(
                 cols = slice(e * C - lo, (e + 1) * C - lo)
                 operand[a, e] = (codes[:, cols].bitcast(FP8X4), plane[:, cols])
 
-        def product(e, a):
-            if a == 0:
-                w = w8[:, 512 * e : 512 * (e + 1)].bitcast(FP8X4)
-                plane = w8_plane
-            else:
-                w = w4[:, 256 * e : 256 * (e + 1)].bitcast(FP4X4)
-                plane = w4_plane
-            nc.tensor.matmul_mx(
-                out=sums(e),
-                lhsT=w,
-                lhsT_scale=plane[:, e * N : (e + 1) * N],
-                rhs=operand[a, e][0],
-                rhs_scale=operand[a, e][1],
-                start=(a == 0),
-                stop=(a == 1),
-            )
-
-        def finish(lo, hi):
+        def products(a, lo, hi):
             for e in range(lo // C, hi // C):
-                product(e, 1)
-                nc.scalar.activation(y[:, e * C : (e + 1) * C], sums(e), GELU, bias=bias[:, e : e + 1])
-
-        def scatter(lo, hi):
-            nc.vector.tensor_tensor(routed[:].indirect(offsets[:, lo // 16 : hi // 16]), y[:, lo:hi], gates[:, lo:hi], MULT)
+                if a == 0:
+                    w, w_plane = w8[:, 512 * e : 512 * (e + 1)].bitcast(FP8X4), w8_plane
+                else:
+                    w, w_plane = w4[:, 256 * e : 256 * (e + 1)].bitcast(FP4X4), w4_plane
+                nc.tensor.matmul_mx(
+                    out=banks[e][:, :C],
+                    lhsT=w,
+                    lhsT_scale=w_plane[:, e * N : (e + 1) * N],
+                    rhs=operand[a, e][0],
+                    rhs_scale=operand[a, e][1],
+                    start=(a == 0),
+                    stop=(a == 1),
+                )
+                if a == 1:
+                    nc.scalar.activation(y[:, e * C : (e + 1) * C], banks[e][:, :C], GELU, bias=bias[:, e : e + 1])
 
         picked0 = held.tile([P, 2, S], U32, name="picked0", align_bytes=64)
-        picked1 = [reuse.tile([P, 2, HALF], U32, name=f"picked1_{h}", align_bytes=64, offset=spare + h * 4096) for h in range(2)]
-        cast(0)
-        cast(1)
+        picked1_at = [spare + h * 2 * HALF * 4 for h in range(2)]
+        picked1 = [
+            reuse.tile([P, 2, HALF], U32, name=f"picked1_{h}", align_bytes=64, offset=picked1_at[h]) for h in range(2)
+        ]
+
+        round_pair(0)
         gather(0, 0, S, picked0[:, 0, :])
-        cast(2)
-        cast(3)
+        round_pair(1)
         for h in range(2):
             gather(1, h * HALF, (h + 1) * HALF, picked0[:, 1, h * HALF : (h + 1) * HALF])
-        cast(4)
-        cast(5)
+        round_pair(2)
         for h in range(2):
             gather(2, h * HALF, (h + 1) * HALF, picked1[h][:, 0, :])
-        first = reuse.tile([P, HALF, 2], U32, name="first", align_bytes=64, offset=4 * RAW)
-        weave(first[:], picked0[:, :, :HALF], "scalar")
-        cast(6)
-        cast(7)
-        early = reuse.tile([P, HALF], U8, name="early", align_bytes=64, offset=6 * RAW)
-        quantise(0, 0, HALF, first[:], early)
-        cast(8)
-        second = reuse.tile([P, HALF, 2], U32, name="second", align_bytes=64, offset=4 * RAW)
-        woven = [held.tile([P, HALF, 2], U32, name=f"last{h}", align_bytes=64) for h in range(2)]
-        for part in range(4):
-            h, lo = part // 2, (part % 2) * 256
-            gather(3, part * 256, (part + 1) * 256, picked1[h][:, 1, lo : lo + 256])
-        weave(second[:, :256, :], picked0[:, :, HALF:768], "scalar")
-        weave(second[:, 256:, :], picked0[:, :, 768:], "gpsimd")
-        for part in range(4):
-            h, lo = part // 2, (part % 2) * 256
-            weave(woven[h][:, lo : lo + 256, :], picked1[h][:, :, lo : lo + 256])
-        for e in range(0, 4):
-            product(e, 0)
-        for lo in (0, 256):
-            quantise(1, lo, lo + 256, woven[0][:, lo : lo + 256, :])
-            finish(lo, lo + 256)
-        late = reuse.tile([P, HALF], U8, name="late", align_bytes=64, offset=spare)
-        quantise(0, HALF, S, second[:], late)
-        for e in range(4, 8):
-            product(e, 0)
-        for lo in (0, 256):
-            quantise(1, HALF + lo, HALF + lo + 256, woven[1][:, lo : lo + 256, :])
-            finish(HALF + lo, HALF + lo + 256)
 
-        for lo, hi in ((0, 256), (256, S)):
-            scatter(lo, hi)
-        edges = (0, 256, 512, 768, 1024, 1280)
-        for lo, hi in zip(edges, edges[1:]):
-            nc.vector.tensor_tensor(total[:, lo:hi], resid[:, lo:hi], routed[:, lo:hi], ADD)
-            nc.sync.dma_start(out[:, lo:hi], total[:, lo:hi])
+        woven0_at = raw_at[2][1]
+        woven0_first = reuse.tile([P, HALF, 2], U32, name="woven0_first", align_bytes=64, offset=woven0_at)
+        weave_on_scalar(woven0_first[:], picked0[:, :, :HALF])
+        round_load(3, 0)
+        round_load(3, 1)
+        plane0_first = reuse.tile([P, HALF], U8, name="plane0_first", align_bytes=64, offset=raw_at[3][1])
+        quantise(0, 0, HALF, woven0_first[:], plane0_first)
+        round_load(3, 2)
+
+        woven0_second = reuse.tile([P, HALF, 2], U32, name="woven0_second", align_bytes=64, offset=woven0_at)
+        woven1 = [held.tile([P, HALF, 2], U32, name=f"woven1_{h}", align_bytes=64) for h in range(2)]
+        quarters = [(lo, lo // HALF, slice(lo % HALF, lo % HALF + QUARTER)) for lo in range(0, S, QUARTER)]
+        for lo, h, cols in quarters:
+            gather(3, lo, lo + QUARTER, picked1[h][:, 1, cols])
+        weave_on_scalar(woven0_second[:, :QUARTER, :], picked0[:, :, HALF : HALF + QUARTER])
+        weave_on_gpsimd(woven0_second[:, QUARTER:, :], picked0[:, :, HALF + QUARTER :])
+        for lo, h, cols in quarters:
+            weave_on_scalar(woven1[h][:, cols, :], picked1[h][:, :, cols])
+
+        products(0, 0, HALF)
+        for lo, h, cols in quarters[:2]:
+            quantise(1, lo, lo + QUARTER, woven1[h][:, cols, :])
+            products(1, lo, lo + QUARTER)
+        for i, (lo, h, cols) in enumerate(quarters[2:]):
+            plane0 = reuse.tile([P, QUARTER], U8, name=f"plane0_{lo}", align_bytes=64, offset=picked1_at[i])
+            quantise(0, lo, lo + QUARTER, woven0_second[:, cols, :], plane0)
+            quantise(1, lo, lo + QUARTER, woven1[h][:, cols, :])
+            products(0, lo, lo + QUARTER)
+            products(1, lo, lo + QUARTER)
+
+        for lo, hi in ((0, QUARTER), (QUARTER, S)):
+            slots = offsets[:, lo // 16 : hi // 16]
+            nc.vector.tensor_tensor(routed[:].indirect(slots), y[:, lo:hi], gates[:, lo:hi], MULT)
+        for lo in range(0, T, STORE):
+            cols = slice(lo, lo + STORE)
+            nc.vector.tensor_tensor(total[:, cols], resid[:, cols], routed[:, cols], ADD)
+            nc.sync.dma_start(out[:, cols], total[:, cols])

@@ -17,7 +17,7 @@ STORE = 256
 STAGGERED = (0, 1)
 CUTS = ((704,), (640,), (512, 960), (512, 960))
 SHARES = (
-    (("vector", 2 / 3), ("vector", 2 / 3)),
+    (("vector", 5 / 7), ("vector", 5 / 7)),
     (("gpsimd", 1 / 2), ("vector", 4 / 9)),
     (("gpsimd", 3 / 7), ("gpsimd", 3 / 7), ("gpsimd", 3 / 7)),
     (("gpsimd", 1 / 2), ("gpsimd", 1 / 2), ("gpsimd", 0)),
@@ -236,4 +236,5 @@ def tile_moe_res_lin_gelu_kernel(
         for lo in range(0, T, STORE):
             cols = slice(lo, lo + STORE)
             nc.vector.tensor_tensor(total[:, cols], resid[:, cols], routed[:, cols], ADD)
-            nc.sync.dma_start(out[:, cols], total[:, cols])
+            queue = nc.scalar if lo // STORE % 2 else nc.sync
+            queue.dma_start(out[:, cols], total[:, cols])

@@ -10,7 +10,7 @@ P = 128
 HALF = S // 2
 QUARTER = S // 4
 GATHER_WINDOW = 1408
-SCATTER_WINDOW = 1536
+SPLIT = 608
 RAW = 2 * T * 4
 STORE = 256
 
@@ -57,7 +57,10 @@ def tile_moe_res_lin_gelu_kernel(
         gates = held.tile([P, S], F32, name="gates")
         resid = held.tile([P, T], F32, name="resid")
         y = held.tile([P, S], F32, name="y")
-        routed = held.tile([P, SCATTER_WINDOW], F32, name="routed")
+        gated = held.tile([P, SPLIT], F32, name="gated")
+        routed_s = held.tile([P, T], F32, name="routed_s")
+        routed_v = held.tile([P, T], F32, name="routed_v")
+        partial = held.tile([P, T], F32, name="partial")
         total = held.tile([P, T], F32, name="total")
         warm = held.tile([P, 8], F32, name="warm")
         banks = [psum.tile([P, 512], F32, name=f"bank{e}") for e in range(E)]
@@ -66,7 +69,8 @@ def tile_moe_res_lin_gelu_kernel(
         nc.gpsimd.memset(pairs[0][:, T:].bitcast(I32), 0)
         nc.gpsimd.memset(w8_plane[:].bitcast(I32), 0)
         nc.gpsimd.memset(w4_plane[:].bitcast(I32), 0)
-        nc.gpsimd.memset(routed[:, :T], 0.0)
+        nc.gpsimd.memset(routed_s[:], 0.0)
+        nc.vector.memset(routed_v[:], 0.0)
         nc.scalar.activation(warm[:], warm[:], GELU)
 
         x_columns = xT.rearrange("(a p u j) w -> a u p j w", a=2, p=P, u=2, j=2)
@@ -112,9 +116,9 @@ def tile_moe_res_lin_gelu_kernel(
         load_scales(w8_plane, w8_scales, range(2, 4))
         load_scales(w4_plane, w4_scales, range(0, 4))
         nc.sync.dma_start(bias[:], b)
-        nc.sync.dma_start(gates[:, :QUARTER], gate[:, :QUARTER])
+        nc.sync.dma_start(gates[:, :HALF], gate[:, :HALF])
         load_words(E // 2, E)
-        nc.sync.dma_start(gates[:, QUARTER:], gate[:, QUARTER:])
+        nc.sync.dma_start(gates[:, HALF:], gate[:, HALF:])
         nc.sync.dma_start(resid[:], xr)
 
         def round_load(q, i):
@@ -230,11 +234,14 @@ def tile_moe_res_lin_gelu_kernel(
             products(0, lo, lo + QUARTER)
             products(1, lo, lo + QUARTER)
 
-        for lo, hi in ((0, QUARTER), (QUARTER, S)):
-            slots = offsets[:, lo // 16 : hi // 16]
-            nc.vector.tensor_tensor(routed[:].indirect(slots), y[:, lo:hi], gates[:, lo:hi], MULT)
+        for lo, hi in ((0, HALF), (HALF, SPLIT)):
+            nc.vector.tensor_tensor(gated[:, lo:hi], y[:, lo:hi], gates[:, lo:hi], MULT)
+        nc.vector.tensor_tensor(routed_v[:].indirect(offsets[:, SPLIT // 16 :]), y[:, SPLIT:], gates[:, SPLIT:], MULT)
+        for lo, hi in ((320, SPLIT), (0, 320)):
+            nc.scalar.activation(routed_s[:].indirect(offsets[:, lo // 16 : hi // 16]), gated[:, lo:hi], COPY)
+        nc.vector.tensor_tensor(partial[:], resid[:], routed_v[:], ADD)
         for lo in range(0, T, STORE):
             cols = slice(lo, lo + STORE)
-            nc.vector.tensor_tensor(total[:, cols], resid[:, cols], routed[:, cols], ADD)
+            nc.vector.tensor_tensor(total[:, cols], partial[:, cols], routed_s[:, cols], ADD)
             queue = nc.scalar if lo // STORE % 2 else nc.sync
             queue.dma_start(out[:, cols], total[:, cols])

@@ -10,7 +10,7 @@ P = 128
 HALF = S // 2
 QUARTER = S // 4
 GATHER_WINDOW = 1408
-SPLIT = 608
+SCALAR_SLOTS = (160, 384, 608)
 RAW = 2 * T * 4
 STORE = 256
 
@@ -57,7 +57,7 @@ def tile_moe_res_lin_gelu_kernel(
         gates = held.tile([P, S], F32, name="gates")
         resid = held.tile([P, T], F32, name="resid")
         y = held.tile([P, S], F32, name="y")
-        gated = held.tile([P, SPLIT], F32, name="gated")
+        gated = held.tile([P, S], F32, name="gated")
         routed_s = held.tile([P, T], F32, name="routed_s")
         routed_v = held.tile([P, T], F32, name="routed_v")
         partial = held.tile([P, T], F32, name="partial")
@@ -116,9 +116,9 @@ def tile_moe_res_lin_gelu_kernel(
         load_scales(w8_plane, w8_scales, range(2, 4))
         load_scales(w4_plane, w4_scales, range(0, 4))
         nc.sync.dma_start(bias[:], b)
-        nc.sync.dma_start(gates[:, :HALF], gate[:, :HALF])
+        nc.sync.dma_start(gates[:, :QUARTER], gate[:, :QUARTER])
         load_words(E // 2, E)
-        nc.sync.dma_start(gates[:, HALF:], gate[:, HALF:])
+        nc.sync.dma_start(gates[:, QUARTER:], gate[:, QUARTER:])
         nc.sync.dma_start(resid[:], xr)
 
         def round_load(q, i):
@@ -234,10 +234,15 @@ def tile_moe_res_lin_gelu_kernel(
             products(0, lo, lo + QUARTER)
             products(1, lo, lo + QUARTER)
 
-        for lo, hi in ((0, HALF), (HALF, SPLIT)):
-            nc.vector.tensor_tensor(gated[:, lo:hi], y[:, lo:hi], gates[:, lo:hi], MULT)
-        nc.vector.tensor_tensor(routed_v[:].indirect(offsets[:, SPLIT // 16 :]), y[:, SPLIT:], gates[:, SPLIT:], MULT)
-        for lo, hi in ((320, SPLIT), (0, 320)):
+        def scatter_on_vector(lo, hi):
+            slots = offsets[:, lo // 16 : hi // 16]
+            nc.vector.tensor_tensor(routed_v[:].indirect(slots), y[:, lo:hi], gates[:, lo:hi], MULT)
+
+        first, middle, last = SCALAR_SLOTS
+        scatter_on_vector(0, first)
+        nc.vector.tensor_tensor(gated[:, first:last], y[:, first:last], gates[:, first:last], MULT)
+        scatter_on_vector(last, S)
+        for lo, hi in ((first, middle), (middle, last)):
             nc.scalar.activation(routed_s[:].indirect(offsets[:, lo // 16 : hi // 16]), gated[:, lo:hi], COPY)
         nc.vector.tensor_tensor(partial[:], resid[:], routed_v[:], ADD)
         for lo in range(0, T, STORE):

@@ -10,7 +10,7 @@ P = 128
 HALF = S // 2
 QUARTER = S // 4
 GATHER_WINDOW = 1408
-SCALAR_SLOTS = (160, 384, 608)
+SCATTER_CUTS = (160, 416, 768)
 RAW = 2 * T * 4
 STORE = 256
 
@@ -116,9 +116,9 @@ def tile_moe_res_lin_gelu_kernel(
         load_scales(w8_plane, w8_scales, range(2, 4))
         load_scales(w4_plane, w4_scales, range(0, 4))
         nc.sync.dma_start(bias[:], b)
-        nc.sync.dma_start(gates[:, :QUARTER], gate[:, :QUARTER])
+        nc.sync.dma_start(gates[:, : SCATTER_CUTS[1]], gate[:, : SCATTER_CUTS[1]])
         load_words(E // 2, E)
-        nc.sync.dma_start(gates[:, QUARTER:], gate[:, QUARTER:])
+        nc.sync.dma_start(gates[:, SCATTER_CUTS[1] :], gate[:, SCATTER_CUTS[1] :])
         nc.sync.dma_start(resid[:], xr)
 
         def round_load(q, i):
@@ -218,8 +218,8 @@ def tile_moe_res_lin_gelu_kernel(
         quarters = [(lo, lo // HALF, slice(lo % HALF, lo % HALF + QUARTER)) for lo in range(0, S, QUARTER)]
         for lo, h, cols in quarters:
             gather(3, lo, lo + QUARTER, picked1[h][:, 1, cols])
-        weave_on_scalar(woven0_second[:, :QUARTER, :], picked0[:, :, HALF : HALF + QUARTER])
-        weave_on_gpsimd(woven0_second[:, QUARTER:, :], picked0[:, :, HALF + QUARTER :])
+        weave_on_scalar(woven0_second[:, :C, :], picked0[:, :, HALF : HALF + C])
+        weave_on_gpsimd(woven0_second[:, C:, :], picked0[:, :, HALF + C :])
         for lo, h, cols in quarters:
             weave_on_scalar(woven1[h][:, cols, :], picked1[h][:, :, cols])
 
@@ -238,11 +238,15 @@ def tile_moe_res_lin_gelu_kernel(
             slots = offsets[:, lo // 16 : hi // 16]
             nc.vector.tensor_tensor(routed_v[:].indirect(slots), y[:, lo:hi], gates[:, lo:hi], MULT)
 
-        first, middle, last = SCALAR_SLOTS
-        scatter_on_vector(0, first)
-        nc.vector.tensor_tensor(gated[:, first:last], y[:, first:last], gates[:, first:last], MULT)
-        scatter_on_vector(last, S)
-        for lo, hi in ((first, middle), (middle, last)):
+        def apply_gate(lo, hi):
+            nc.vector.tensor_tensor(gated[:, lo:hi], y[:, lo:hi], gates[:, lo:hi], MULT)
+
+        first, second, third = SCATTER_CUTS
+        apply_gate(0, first)
+        scatter_on_vector(first, second)
+        apply_gate(second, third)
+        scatter_on_vector(third, S)
+        for lo, hi in ((0, first), (second, third)):
             nc.scalar.activation(routed_s[:].indirect(offsets[:, lo // 16 : hi // 16]), gated[:, lo:hi], COPY)
         nc.vector.tensor_tensor(partial[:], resid[:], routed_v[:], ADD)
         for lo in range(0, T, STORE):

@@ -116,8 +116,8 @@ def tile_moe_res_lin_gelu_kernel(
         load_scales(w8_plane, w8_scales, range(2, 4))
         load_scales(w4_plane, w4_scales, range(0, 4))
         nc.sync.dma_start(bias[:], b)
-        nc.sync.dma_start(gates[:, : SCATTER_CUTS[1]], gate[:, : SCATTER_CUTS[1]])
         load_words(E // 2, E)
+        nc.sync.dma_start(gates[:, : SCATTER_CUTS[1]], gate[:, : SCATTER_CUTS[1]])
         nc.sync.dma_start(gates[:, SCATTER_CUTS[1] :], gate[:, SCATTER_CUTS[1] :])
         nc.sync.dma_start(resid[:], xr)
 
@@ -248,7 +248,9 @@ def tile_moe_res_lin_gelu_kernel(
         scatter_on_vector(third, S)
         for lo, hi in ((0, first), (second, third)):
             nc.scalar.activation(routed_s[:].indirect(offsets[:, lo // 16 : hi // 16]), gated[:, lo:hi], COPY)
-        nc.vector.tensor_tensor(partial[:], resid[:], routed_v[:], ADD)
+        for lo in range(0, T, STORE):
+            cols = slice(lo, lo + STORE)
+            nc.vector.tensor_tensor(partial[:, cols], resid[:, cols], routed_v[:, cols], ADD)
         for lo in range(0, T, STORE):
             cols = slice(lo, lo + STORE)
             nc.vector.tensor_tensor(total[:, cols], partial[:, cols], routed_s[:, cols], ADD)

@@ -10,7 +10,7 @@ P = 128
 HALF = S // 2
 QUARTER = S // 4
 GATHER_WINDOW = 1408
-SCATTER_CUTS = (160, 416, 768)
+SCATTER_CUTS = (160, 384, 768)
 RAW = 2 * T * 4
 STORE = 256
 

@@ -9,20 +9,9 @@ FLOPS = 2 * S * K * N
 P = 128
 HALF = S // 2
 QUARTER = S // 4
-GATHER_WINDOW = 1408
-SCATTER_CUTS = (160, 384, 768)
-RAW = 2 * T * 4
 STORE = 256
-
-STAGGERED = (0, 1)
-CUTS = ((704,), (640,), (512, 960), (512, 960))
-SHARES = (
-    (("vector", 5 / 7), ("vector", 5 / 7)),
-    (("gpsimd", 1 / 2), ("vector", 4 / 9)),
-    (("gpsimd", 3 / 7), ("gpsimd", 3 / 7), ("gpsimd", 3 / 7)),
-    (("gpsimd", 1 / 2), ("gpsimd", 1 / 2), ("gpsimd", 0)),
-)
-SHARE_STEP = 32
+SCALAR_LACES = (256, 672)
+SCATTER_CUTS = (160, 384, 768)
 
 F32 = mybir.dt.float32
 BF16 = mybir.dt.bfloat16
@@ -48,7 +37,6 @@ def tile_moe_res_lin_gelu_kernel(
         psum = ctx.enter_context(tc.psum_pool(name="psum", bufs=1))
 
         offsets = held.tile([P, S // 16], U16, name="offsets")
-        pairs = [held.tile([P, GATHER_WINDOW if q == 0 else T], U32, name=f"pairs{q}", align_bytes=64) for q in range(4)]
         w8 = held.tile([P, E * 512], U8, name="w8", align_bytes=64)
         w4 = held.tile([P, E * 256], U8, name="w4", align_bytes=64)
         w8_plane = held.tile([P, E * N], U8, name="w8_plane", align_bytes=64)
@@ -66,39 +54,24 @@ def tile_moe_res_lin_gelu_kernel(
         banks = [psum.tile([P, 512], F32, name=f"bank{e}") for e in range(E)]
 
         nc.gpsimd.memset(warm[:], 0.0)
-        nc.gpsimd.memset(pairs[0][:, T:].bitcast(I32), 0)
         nc.gpsimd.memset(w8_plane[:].bitcast(I32), 0)
         nc.gpsimd.memset(w4_plane[:].bitcast(I32), 0)
         nc.gpsimd.memset(routed_s[:], 0.0)
         nc.vector.memset(routed_v[:], 0.0)
         nc.scalar.activation(warm[:], warm[:], GELU)
 
-        x_columns = xT.rearrange("(a p u j) w -> a u p j w", a=2, p=P, u=2, j=2)
-        x_runs = xT.rearrange("(a p u j) w -> a u p (j w)", a=2, p=P, u=2, j=2)
+        x_rows = xT.rearrange("(a p t) w -> a t p w", a=2, p=P, t=4)
         w8_view = w8_words.rearrange("e a p n r -> p (e a) (n r)").bitcast(I32)
         w4_view = w4_words.rearrange("e a p n -> p (e a) n").bitcast(I32)
         w8_i = w8[:].bitcast(I32).rearrange("p (e n) -> p e n", e=E)
         w4_i = w4[:].bitcast(I32).rearrange("p (e n) -> p e n", e=E)
 
-        edges = [(0, *cuts, T) for cuts in CUTS]
-        raw = [[] for q in range(4)]
-        raw_at = [[] for q in range(4)]
-        spare = 0
-        for q in range(4):
-            for lo, hi in zip(edges[q], edges[q][1:]):
-                if q in STAGGERED:
-                    if lo == 0:
-                        run = reuse.tile([P, 2 * T], F32, name=f"raw{q}", align_bytes=64, offset=spare)
-                    begin = 0 if lo == 0 else T + lo
-                    nc.sync.dma_start(run[:, begin : T + hi], x_runs[q // 2, q % 2][:, begin : T + hi])
-                    raw[q].append(run[:].rearrange("p (j w) -> p j w", j=2)[:, :, lo:hi])
-                else:
-                    piece = reuse.tile([P, 2, hi - lo], F32, name=f"raw{q}_{lo}", align_bytes=64, offset=spare)
-                    nc.sync.dma_start(piece[:], x_columns[q // 2, q % 2][:, :, lo:hi])
-                    raw[q].append(piece[:])
-                raw_at[q].append(spare)
-                spare += RAW
-            if q == 0:
+        rows = []
+        for r in range(8):
+            row = reuse.tile([P, T], F32, name=f"row{r}", align_bytes=64, offset=r * T * 4)
+            nc.sync.dma_start(row[:], x_rows[r // 4, r % 4])
+            rows.append(row)
+            if r == 0:
                 nc.sync.dma_start(offsets[:], offs)
 
         def load_scales(plane, scales, rows):
@@ -121,52 +94,36 @@ def tile_moe_res_lin_gelu_kernel(
         nc.sync.dma_start(gates[:, SCATTER_CUTS[1] :], gate[:, SCATTER_CUTS[1] :])
         nc.sync.dma_start(resid[:], xr)
 
-        def round_load(q, i):
-            lo, hi = edges[q][i], edges[q][i + 1]
-            helper, share = SHARES[q][i]
-            cut = round((hi - lo) * share / SHARE_STEP) * SHARE_STEP
-            for engine, first, last in ((helper, 0, cut), ("scalar", cut, hi - lo)):
-                if first == last:
-                    continue
-                dst = pairs[q][:, lo + first : lo + last].bitcast(BF16).rearrange("p (w j) -> p w j", j=2)
-                src = raw[q][i][:, :, first:last].rearrange("p j w -> p w j")
-                if engine == "gpsimd":
-                    nc.gpsimd.tensor_scalar(dst, src, 1.0, 0.0, MULT, ADD)
-                    continue
-                dst = dst.rearrange("p (c i) j -> p c j i", i=4)
-                src = src.rearrange("p (c i) j -> p c j i", i=4)
-                if engine == "vector":
-                    nc.vector.tensor_copy(dst, src)
-                else:
-                    nc.scalar.activation(dst, src, COPY)
+        picked = [held.tile([P, 4, S], BF16, name=f"picked{a}", align_bytes=64) for a in range(2)]
+        woven = [held.tile([P, S, 4], BF16, name=f"woven{a}", align_bytes=64) for a in range(2)]
 
-        def round_pair(q):
-            for i in range(len(raw[q])):
-                round_load(q, i)
+        def gather_row(r):
+            window, dst = rows[r][:], picked[r // 4][:, r % 4, :]
+            cuts = (0, QUARTER, HALF) if r % 4 == 3 else (0, HALF)
+            for lo, hi in zip(cuts, cuts[1:]):
+                nc.vector.tensor_copy(dst[:, lo:hi], window.indirect(offsets[:, lo // 16 : hi // 16]))
+            nc.scalar.activation(dst[:, HALF:], window.indirect(offsets[:, HALF // 16 :]), COPY)
 
-        def gather(q, lo, hi, dst):
-            nc.vector.tensor_copy(dst, pairs[q][:].indirect(offsets[:, lo // 16 : hi // 16]))
-
-        def weave_on_scalar(dst, src):
-            nc.scalar.copy(dst.rearrange("p (c i) u -> p c u i", i=2), src.rearrange("p u (c i) -> p c u i", i=2))
-
-        def weave_on_gpsimd(dst, src):
-            nc.gpsimd.tensor_scalar(
-                dst.bitcast(BF16).rearrange("p c (u j) -> p c u j", j=2),
-                src.bitcast(BF16).rearrange("p u (c j) -> p c u j", j=2),
-                1.0,
-                0.0,
-                MULT,
-                ADD,
-            )
+        def lace(engine, a, lo, hi):
+            dst, src = woven[a][:, lo:hi, :], picked[a][:, :, lo:hi]
+            if engine == "gpsimd":
+                nc.gpsimd.tensor_scalar(dst, src.rearrange("p t c -> p c t"), 1.0, 0.0, MULT, ADD)
+                return
+            dst = dst.rearrange("p (c i) t -> p c t i", i=4)
+            src = src.rearrange("p t (c i) -> p c t i", i=4)
+            if engine == "vector":
+                nc.vector.tensor_copy(dst, src)
+            else:
+                nc.scalar.copy(dst, src)
 
         operand = {}
 
-        def quantise(a, lo, hi, woven, plane=None):
+        def quantise(a, lo, hi, plane=None):
+            source = woven[a][:, lo:hi, :].rearrange("p c t -> p (c t)")
             codes = held.tile([P, hi - lo], U32, name=f"codes{a}_{lo}", align_bytes=64)
             if plane is None:
                 plane = held.tile([P, hi - lo], U8, name=f"plane{a}_{lo}", align_bytes=64)
-            nc.vector.quantize_mx(codes[:].bitcast(FP8X4), plane[:], woven.rearrange("p c u -> p (c u)").bitcast(BF16))
+            nc.vector.quantize_mx(codes[:].bitcast(FP8X4), plane[:], source)
             for e in range(lo // C, hi // C):
                 cols = slice(e * C - lo, (e + 1) * C - lo)
                 operand[a, e] = (codes[:, cols].bitcast(FP8X4), plane[:, cols])
@@ -189,48 +146,29 @@ def tile_moe_res_lin_gelu_kernel(
                 if a == 1:
                     nc.scalar.activation(y[:, e * C : (e + 1) * C], banks[e][:, :C], GELU, bias=bias[:, e : e + 1])
 
-        picked0 = held.tile([P, 2, S], U32, name="picked0", align_bytes=64)
-        picked1_at = [spare + h * 2 * HALF * 4 for h in range(2)]
-        picked1 = [
-            reuse.tile([P, 2, HALF], U32, name=f"picked1_{h}", align_bytes=64, offset=picked1_at[h]) for h in range(2)
+        for r in range(4):
+            gather_row(r)
+        for lo in range(0, S, QUARTER):
+            lace("gpsimd", 0, lo, lo + QUARTER)
+        for r in range(4, 8):
+            gather_row(r)
+
+        planes0 = [
+            reuse.tile([P, HALF], U8, name=f"plane0_{h}", align_bytes=64, offset=7 * T * 4 + h * HALF) for h in range(2)
         ]
-
-        round_pair(0)
-        gather(0, 0, S, picked0[:, 0, :])
-        round_pair(1)
-        for h in range(2):
-            gather(1, h * HALF, (h + 1) * HALF, picked0[:, 1, h * HALF : (h + 1) * HALF])
-        round_pair(2)
-        for h in range(2):
-            gather(2, h * HALF, (h + 1) * HALF, picked1[h][:, 0, :])
-
-        woven0_at = raw_at[2][1]
-        woven0_first = reuse.tile([P, HALF, 2], U32, name="woven0_first", align_bytes=64, offset=woven0_at)
-        weave_on_scalar(woven0_first[:], picked0[:, :, :HALF])
-        round_load(3, 0)
-        round_load(3, 1)
-        plane0_first = reuse.tile([P, HALF], U8, name="plane0_first", align_bytes=64, offset=raw_at[3][1])
-        quantise(0, 0, HALF, woven0_first[:], plane0_first)
-        round_load(3, 2)
-
-        woven0_second = reuse.tile([P, HALF, 2], U32, name="woven0_second", align_bytes=64, offset=woven0_at)
-        woven1 = [held.tile([P, HALF, 2], U32, name=f"woven1_{h}", align_bytes=64) for h in range(2)]
-        quarters = [(lo, lo // HALF, slice(lo % HALF, lo % HALF + QUARTER)) for lo in range(0, S, QUARTER)]
-        for lo, h, cols in quarters:
-            gather(3, lo, lo + QUARTER, picked1[h][:, 1, cols])
-        weave_on_scalar(woven0_second[:, :C, :], picked0[:, :, HALF : HALF + C])
-        weave_on_gpsimd(woven0_second[:, C:, :], picked0[:, :, HALF + C :])
-        for lo, h, cols in quarters:
-            weave_on_scalar(woven1[h][:, cols, :], picked1[h][:, :, cols])
-
+        first, last = SCALAR_LACES
+        lace("vector", 1, 0, first)
+        lace("scalar", 1, first, HALF)
+        lace("scalar", 1, HALF, last)
+        quantise(0, 0, HALF, planes0[0])
         products(0, 0, HALF)
-        for lo, h, cols in quarters[:2]:
-            quantise(1, lo, lo + QUARTER, woven1[h][:, cols, :])
+        for lo in (0, QUARTER):
+            quantise(1, lo, lo + QUARTER)
             products(1, lo, lo + QUARTER)
-        for i, (lo, h, cols) in enumerate(quarters[2:]):
-            plane0 = reuse.tile([P, QUARTER], U8, name=f"plane0_{lo}", align_bytes=64, offset=picked1_at[i])
-            quantise(0, lo, lo + QUARTER, woven0_second[:, cols, :], plane0)
-            quantise(1, lo, lo + QUARTER, woven1[h][:, cols, :])
+        lace("vector", 1, last, S)
+        quantise(0, HALF, S, planes0[1])
+        for lo in (HALF, HALF + QUARTER):
+            quantise(1, lo, lo + QUARTER)
             products(0, lo, lo + QUARTER)
             products(1, lo, lo + QUARTER)
 

@@ -10,7 +10,8 @@ P = 128
 HALF = S // 2
 QUARTER = S // 4
 STORE = 256
-SCALAR_LACES = (256, 672)
+VECTOR_SLOTS = (512, 512, 512, 512, 448, 448, 384, 576)
+SCALAR_LACES = (256, 704)
 SCATTER_CUTS = (160, 384, 768)
 
 F32 = mybir.dt.float32
@@ -73,6 +74,7 @@ def tile_moe_res_lin_gelu_kernel(
             rows.append(row)
             if r == 0:
                 nc.sync.dma_start(offsets[:], offs)
+                nc.sync.dma_start(bias[:], b)
 
         def load_scales(plane, scales, rows):
             src = scales.rearrange("e a q n -> q (e a) n").bitcast(I32)
@@ -84,28 +86,33 @@ def tile_moe_res_lin_gelu_kernel(
             nc.sync.dma_start(w8_i[:, lo:hi, :], w8_view[:, lo:hi, :])
             nc.sync.dma_start(w4_i[:, lo:hi, :], w4_view[:, lo:hi, :])
 
-        load_scales(w8_plane, w8_scales, range(0, 2))
+        load_scales(w8_plane, w8_scales, range(0, 4))
         load_words(0, E // 2)
-        load_scales(w8_plane, w8_scales, range(2, 4))
         load_scales(w4_plane, w4_scales, range(0, 4))
-        nc.sync.dma_start(bias[:], b)
         load_words(E // 2, E)
         nc.sync.dma_start(gates[:, : SCATTER_CUTS[1]], gate[:, : SCATTER_CUTS[1]])
         nc.sync.dma_start(gates[:, SCATTER_CUTS[1] :], gate[:, SCATTER_CUTS[1] :])
         nc.sync.dma_start(resid[:], xr)
 
-        picked = [held.tile([P, 4, S], BF16, name=f"picked{a}", align_bytes=64) for a in range(2)]
-        woven = [held.tile([P, S, 4], BF16, name=f"woven{a}", align_bytes=64) for a in range(2)]
+        picked_at = [8 * T * 4 + a * 4 * S * 2 for a in range(2)]
+        picked = [reuse.tile([P, 4, S], BF16, name=f"picked{a}", align_bytes=64, offset=picked_at[a]) for a in range(2)]
+        woven_at = picked_at[1] + 4 * S * 2
+        woven0_first = reuse.tile([P, HALF, 4], BF16, name="woven0_first", align_bytes=64, offset=woven_at)
+        woven1 = held.tile([P, S, 4], BF16, name="woven1", align_bytes=64)
 
         def gather_row(r):
             window, dst = rows[r][:], picked[r // 4][:, r % 4, :]
-            cuts = (0, QUARTER, HALF) if r % 4 == 3 else (0, HALF)
+            cut = VECTOR_SLOTS[r]
+            cuts = (0, QUARTER, cut) if r % 4 == 3 else (0, cut)
             for lo, hi in zip(cuts, cuts[1:]):
                 nc.vector.tensor_copy(dst[:, lo:hi], window.indirect(offsets[:, lo // 16 : hi // 16]))
-            nc.scalar.activation(dst[:, HALF:], window.indirect(offsets[:, HALF // 16 :]), COPY)
+            nc.scalar.activation(dst[:, cut:], window.indirect(offsets[:, cut // 16 :]), COPY)
 
-        def lace(engine, a, lo, hi):
-            dst, src = woven[a][:, lo:hi, :], picked[a][:, :, lo:hi]
+        def lace_two(t, lo, hi):
+            src = picked[0][:, t : t + 2, lo:hi].rearrange("p t c -> p c t")
+            nc.gpsimd.tensor_scalar(woven0_first[:, lo:hi, t : t + 2], src, 1.0, 0.0, MULT, ADD)
+
+        def lace(engine, dst, src):
             if engine == "gpsimd":
                 nc.gpsimd.tensor_scalar(dst, src.rearrange("p t c -> p c t"), 1.0, 0.0, MULT, ADD)
                 return
@@ -118,8 +125,8 @@ def tile_moe_res_lin_gelu_kernel(
 
         operand = {}
 
-        def quantise(a, lo, hi, plane=None):
-            source = woven[a][:, lo:hi, :].rearrange("p c t -> p (c t)")
+        def quantise(a, lo, hi, woven, plane=None):
+            source = woven.rearrange("p c t -> p (c t)")
             codes = held.tile([P, hi - lo], U32, name=f"codes{a}_{lo}", align_bytes=64)
             if plane is None:
                 plane = held.tile([P, hi - lo], U8, name=f"plane{a}_{lo}", align_bytes=64)
@@ -148,28 +155,37 @@ def tile_moe_res_lin_gelu_kernel(
 
         for r in range(4):
             gather_row(r)
-        for lo in range(0, S, QUARTER):
-            lace("gpsimd", 0, lo, lo + QUARTER)
-        for r in range(4, 8):
-            gather_row(r)
-
-        planes0 = [
-            reuse.tile([P, HALF], U8, name=f"plane0_{h}", align_bytes=64, offset=7 * T * 4 + h * HALF) for h in range(2)
-        ]
-        first, last = SCALAR_LACES
-        lace("vector", 1, 0, first)
-        lace("scalar", 1, first, HALF)
-        lace("scalar", 1, HALF, last)
-        quantise(0, 0, HALF, planes0[0])
-        products(0, 0, HALF)
+            if r == 1:
+                lace_two(0, 0, HALF)
         for lo in (0, QUARTER):
-            quantise(1, lo, lo + QUARTER)
-            products(1, lo, lo + QUARTER)
-        lace("vector", 1, last, S)
-        quantise(0, HALF, S, planes0[1])
-        for lo in (HALF, HALF + QUARTER):
-            quantise(1, lo, lo + QUARTER)
-            products(0, lo, lo + QUARTER)
+            lace_two(2, lo, lo + QUARTER)
+        gather_row(4)
+        quantise(0, 0, HALF, woven0_first[:])
+        woven0_third = reuse.tile([P, QUARTER, 4], BF16, name="woven0_third", align_bytes=64, offset=woven_at)
+        lace("gpsimd", woven0_third[:], picked[0][:, :, HALF : HALF + QUARTER])
+        gather_row(5)
+        gather_row(6)
+        quantise(0, HALF, HALF + QUARTER, woven0_third[:])
+        woven0_last = reuse.tile([P, QUARTER, 4], BF16, name="woven0_last", align_bytes=64, offset=woven_at)
+        lace("gpsimd", woven0_last[:], picked[0][:, :, HALF + QUARTER :])
+        gather_row(7)
+
+        def lace_second_pass(engine, lo, hi):
+            lace(engine, woven1[:, lo:hi, :], picked[1][:, :, lo:hi])
+
+        first, last = SCALAR_LACES
+        lace_second_pass("vector", 0, first)
+        lace_second_pass("scalar", first, HALF)
+        lace_second_pass("scalar", HALF, last)
+        plane0_last = reuse.tile([P, QUARTER], U8, name="plane0_last", align_bytes=64, offset=7 * T * 4)
+        lace_second_pass("vector", last, S)
+        for lo in range(0, S, QUARTER):
+            if lo == HALF:
+                quantise(0, HALF + QUARTER, S, woven0_last[:], plane0_last)
+                products(0, HALF, S)
+            quantise(1, lo, lo + QUARTER, woven1[:, lo : lo + QUARTER, :])
+            if lo == 0:
+                products(0, 0, HALF)
             products(1, lo, lo + QUARTER)
 
         def scatter_on_vector(lo, hi):

from contextlib import ExitStack

import concourse.mybir as mybir

K, T, E, C, N = 1024, 1280, 8, 128, 128
S = E * C
FLOPS = 2 * S * K * N

P = 128
HALF = S // 2
QUARTER = S // 4
STORE = 256
VECTOR_SLOTS = (512, 512, 512, 512, 448, 448, 384, 576)
SCALAR_LACES = (256, 704)
SCATTER_CUTS = (160, 384, 768)

F32 = mybir.dt.float32
BF16 = mybir.dt.bfloat16
I32 = mybir.dt.int32
U32 = mybir.dt.uint32
U16 = mybir.dt.uint16
U8 = mybir.dt.uint8
FP8X4 = mybir.dt.float8_e4m3fn_x4
FP4X4 = mybir.dt.float4_e2m1fn_x4
COPY = mybir.ActivationFunctionType.Copy
GELU = mybir.ActivationFunctionType.Gelu_apprx_tanh
ADD = mybir.AluOpType.add
MULT = mybir.AluOpType.mult


def tile_moe_res_lin_gelu_kernel(
    tc, xT, xr, w8_words, w8_scales, w4_words, w4_scales, b, gate, offs, out
):
    nc = tc.nc
    with ExitStack() as ctx:
        held = ctx.enter_context(tc.tile_pool(name="held", bufs=1))
        reuse = ctx.enter_context(tc.tile_pool(name="reuse", bufs=1))
        psum = ctx.enter_context(tc.psum_pool(name="psum", bufs=1))

        offsets = held.tile([P, S // 16], U16, name="offsets")
        w8 = held.tile([P, E * 512], U8, name="w8", align_bytes=64)
        w4 = held.tile([P, E * 256], U8, name="w4", align_bytes=64)
        w8_plane = held.tile([P, E * N], U8, name="w8_plane", align_bytes=64)
        w4_plane = held.tile([P, E * N], U8, name="w4_plane", align_bytes=64)
        bias = held.tile([P, E], F32, name="bias")
        gates = held.tile([P, S], F32, name="gates")
        resid = held.tile([P, T], F32, name="resid")
        y = held.tile([P, S], F32, name="y")
        gated = held.tile([P, S], F32, name="gated")
        routed_s = held.tile([P, T], F32, name="routed_s")
        routed_v = held.tile([P, T], F32, name="routed_v")
        partial = held.tile([P, T], F32, name="partial")
        total = held.tile([P, T], F32, name="total")
        warm = held.tile([P, 8], F32, name="warm")
        banks = [psum.tile([P, 512], F32, name=f"bank{e}") for e in range(E)]

        nc.gpsimd.memset(warm[:], 0.0)
        nc.gpsimd.memset(w8_plane[:].bitcast(I32), 0)
        nc.gpsimd.memset(w4_plane[:].bitcast(I32), 0)
        nc.gpsimd.memset(routed_s[:], 0.0)
        nc.vector.memset(routed_v[:], 0.0)
        nc.scalar.activation(warm[:], warm[:], GELU)

        x_rows = xT.rearrange("(a p t) w -> a t p w", a=2, p=P, t=4)
        w8_view = w8_words.rearrange("e a p n r -> p (e a) (n r)").bitcast(I32)
        w4_view = w4_words.rearrange("e a p n -> p (e a) n").bitcast(I32)
        w8_i = w8[:].bitcast(I32).rearrange("p (e n) -> p e n", e=E)
        w4_i = w4[:].bitcast(I32).rearrange("p (e n) -> p e n", e=E)

        rows = []
        for r in range(8):
            row = reuse.tile([P, T], F32, name=f"row{r}", align_bytes=64, offset=r * T * 4)
            nc.sync.dma_start(row[:], x_rows[r // 4, r % 4])
            rows.append(row)
            if r == 0:
                nc.sync.dma_start(offsets[:], offs)
                nc.sync.dma_start(bias[:], b)

        def load_scales(plane, scales, rows):
            src = scales.rearrange("e a q n -> q (e a) n").bitcast(I32)
            dst = plane[:].bitcast(I32).rearrange("p (e n) -> p e n", e=E)
            for r in rows:
                nc.sync.dma_start(dst[r:P:32], src[r:16:4])

        def load_words(lo, hi):
            nc.sync.dma_start(w8_i[:, lo:hi, :], w8_view[:, lo:hi, :])
            nc.sync.dma_start(w4_i[:, lo:hi, :], w4_view[:, lo:hi, :])

        load_scales(w8_plane, w8_scales, range(0, 4))
        load_words(0, E // 2)
        load_scales(w4_plane, w4_scales, range(0, 4))
        load_words(E // 2, E)
        nc.sync.dma_start(gates[:, : SCATTER_CUTS[1]], gate[:, : SCATTER_CUTS[1]])
        nc.sync.dma_start(gates[:, SCATTER_CUTS[1] :], gate[:, SCATTER_CUTS[1] :])
        nc.sync.dma_start(resid[:], xr)

        picked_at = [8 * T * 4 + a * 4 * S * 2 for a in range(2)]
        picked = [reuse.tile([P, 4, S], BF16, name=f"picked{a}", align_bytes=64, offset=picked_at[a]) for a in range(2)]
        woven_at = picked_at[1] + 4 * S * 2
        woven0_first = reuse.tile([P, HALF, 4], BF16, name="woven0_first", align_bytes=64, offset=woven_at)
        woven1 = held.tile([P, S, 4], BF16, name="woven1", align_bytes=64)

        def gather_row(r):
            window, dst = rows[r][:], picked[r // 4][:, r % 4, :]
            cut = VECTOR_SLOTS[r]
            cuts = (0, QUARTER, cut) if r % 4 == 3 else (0, cut)
            for lo, hi in zip(cuts, cuts[1:]):
                nc.vector.tensor_copy(dst[:, lo:hi], window.indirect(offsets[:, lo // 16 : hi // 16]))
            nc.scalar.activation(dst[:, cut:], window.indirect(offsets[:, cut // 16 :]), COPY)

        def lace_two(t, lo, hi):
            src = picked[0][:, t : t + 2, lo:hi].rearrange("p t c -> p c t")
            nc.gpsimd.tensor_scalar(woven0_first[:, lo:hi, t : t + 2], src, 1.0, 0.0, MULT, ADD)

        def lace(engine, dst, src):
            if engine == "gpsimd":
                nc.gpsimd.tensor_scalar(dst, src.rearrange("p t c -> p c t"), 1.0, 0.0, MULT, ADD)
                return
            dst = dst.rearrange("p (c i) t -> p c t i", i=4)
            src = src.rearrange("p t (c i) -> p c t i", i=4)
            if engine == "vector":
                nc.vector.tensor_copy(dst, src)
            else:
                nc.scalar.copy(dst, src)

        operand = {}

        def quantise(a, lo, hi, woven, plane=None):
            source = woven.rearrange("p c t -> p (c t)")
            codes = held.tile([P, hi - lo], U32, name=f"codes{a}_{lo}", align_bytes=64)
            if plane is None:
                plane = held.tile([P, hi - lo], U8, name=f"plane{a}_{lo}", align_bytes=64)
            nc.vector.quantize_mx(codes[:].bitcast(FP8X4), plane[:], source)
            for e in range(lo // C, hi // C):
                cols = slice(e * C - lo, (e + 1) * C - lo)
                operand[a, e] = (codes[:, cols].bitcast(FP8X4), plane[:, cols])

        def products(a, lo, hi):
            for e in range(lo // C, hi // C):
                if a == 0:
                    w, w_plane = w8[:, 512 * e : 512 * (e + 1)].bitcast(FP8X4), w8_plane
                else:
                    w, w_plane = w4[:, 256 * e : 256 * (e + 1)].bitcast(FP4X4), w4_plane
                nc.tensor.matmul_mx(
                    out=banks[e][:, :C],
                    lhsT=w,
                    lhsT_scale=w_plane[:, e * N : (e + 1) * N],
                    rhs=operand[a, e][0],
                    rhs_scale=operand[a, e][1],
                    start=(a == 0),
                    stop=(a == 1),
                )
                if a == 1:
                    nc.scalar.activation(y[:, e * C : (e + 1) * C], banks[e][:, :C], GELU, bias=bias[:, e : e + 1])

        for r in range(4):
            gather_row(r)
            if r == 1:
                lace_two(0, 0, HALF)
        for lo in (0, QUARTER):
            lace_two(2, lo, lo + QUARTER)
        gather_row(4)
        quantise(0, 0, HALF, woven0_first[:])
        woven0_third = reuse.tile([P, QUARTER, 4], BF16, name="woven0_third", align_bytes=64, offset=woven_at)
        lace("gpsimd", woven0_third[:], picked[0][:, :, HALF : HALF + QUARTER])
        gather_row(5)
        gather_row(6)
        quantise(0, HALF, HALF + QUARTER, woven0_third[:])
        woven0_last = reuse.tile([P, QUARTER, 4], BF16, name="woven0_last", align_bytes=64, offset=woven_at)
        lace("gpsimd", woven0_last[:], picked[0][:, :, HALF + QUARTER :])
        gather_row(7)

        def lace_second_pass(engine, lo, hi):
            lace(engine, woven1[:, lo:hi, :], picked[1][:, :, lo:hi])

        first, last = SCALAR_LACES
        lace_second_pass("vector", 0, first)
        lace_second_pass("scalar", first, HALF)
        lace_second_pass("scalar", HALF, last)
        plane0_last = reuse.tile([P, QUARTER], U8, name="plane0_last", align_bytes=64, offset=7 * T * 4)
        lace_second_pass("vector", last, S)
        for lo in range(0, S, QUARTER):
            if lo == HALF:
                quantise(0, HALF + QUARTER, S, woven0_last[:], plane0_last)
                products(0, HALF, S)
            quantise(1, lo, lo + QUARTER, woven1[:, lo : lo + QUARTER, :])
            if lo == 0:
                products(0, 0, HALF)
            products(1, lo, lo + QUARTER)

        def scatter_on_vector(lo, hi):
            slots = offsets[:, lo // 16 : hi // 16]
            nc.vector.tensor_tensor(routed_v[:].indirect(slots), y[:, lo:hi], gates[:, lo:hi], MULT)

        def apply_gate(lo, hi):
            nc.vector.tensor_tensor(gated[:, lo:hi], y[:, lo:hi], gates[:, lo:hi], MULT)

        first, second, third = SCATTER_CUTS
        apply_gate(0, first)
        scatter_on_vector(first, second)
        apply_gate(second, third)
        scatter_on_vector(third, S)
        for lo, hi in ((0, first), (second, third)):
            nc.scalar.activation(routed_s[:].indirect(offsets[:, lo // 16 : hi // 16]), gated[:, lo:hi], COPY)
        for lo in range(0, T, STORE):
            cols = slice(lo, lo + STORE)
            nc.vector.tensor_tensor(partial[:, cols], resid[:, cols], routed_v[:, cols], ADD)
        for lo in range(0, T, STORE):
            cols = slice(lo, lo + STORE)
            nc.vector.tensor_tensor(total[:, cols], partial[:, cols], routed_s[:, cols], ADD)
            queue = nc.scalar if lo // STORE % 2 else nc.sync
            queue.dma_start(out[:, cols], total[:, cols])
